import numpy as np
import ml_dtypes


def mxq(x, axis, fmt="e4m3"):
    dtype, down = {"e4m3": (ml_dtypes.float8_e4m3fn, 7), "e5m2": (ml_dtypes.float8_e5m2, 14)}[fmt]
    v = np.moveaxis(np.asarray(x, np.float32).astype(ml_dtypes.bfloat16).astype(np.float64), axis, -1)
    blocks = v.reshape(v.shape[:-1] + (-1, 32))
    amax = np.abs(blocks).max(-1, keepdims=True)
    byte = np.maximum(np.where(amax > 0, np.frexp(amax)[1] - 1 + 127, 0) - down, 1)
    scale = np.exp2(byte - 127.0)
    codes = (blocks / scale).astype(np.float32).astype(dtype).astype(np.float64)
    return np.moveaxis((codes * scale).reshape(v.shape), -1, axis)


WIDE = False


def mx_kscale(k):
    if not WIDE:
        return np.ones(k)
    levels = np.array([10, -10, 5, -5, 0])
    if k % 512:
        return np.exp2(np.random.permutation(np.resize(levels, k // 32))).repeat(32)
    a = np.empty((k // 512, 16))
    for p in range(k // 512):
        a[p, :8] = np.random.permutation(np.resize(levels, 8))
        for g in range(8):
            far = levels[np.abs(levels - a[p, g]) >= 10]
            a[p, g + 8] = far[np.random.randint(len(far))]
    return np.exp2(a.ravel()).repeat(32)


def f64(x):
    return np.asarray(x).astype(np.float64)


def striped(idx):
    return np.tile(idx.reshape(-1, 16).T, (8, 1)).astype(np.uint16)


def unstriped(offs):
    return offs[:16].T.reshape(-1).astype(np.int64)


E2M1 = np.array([0.0, 0.5, 1.0, 1.5, 2.0, 3.0, 4.0, 6.0, -0.0, -0.5, -1.0, -1.5, -2.0, -3.0, -4.0, -6.0])


def pack_weight(w, fmt):
    k, n = w.shape
    w = f64(np.asarray(w, np.float32).astype(ml_dtypes.bfloat16)).reshape(k // 32, 32, n)
    amax = np.abs(w).max(1)
    if fmt == "e4m3":
        byte = np.frexp(amax)[1] - 1 + 127 - 7
    else:
        mant, ex = np.frexp(amax / 6.0)
        byte = np.where(mant > 0.5, ex, ex - 1) + 127
    byte = np.clip(np.where(amax > 0, byte, 1), 1, 254)
    scaled = (w * np.exp2(127.0 - byte)[:, None, :]).reshape(k, n).astype(np.float32)
    by_word = np.ascontiguousarray(scaled.reshape(k // 512, 128, 4, n).transpose(0, 1, 3, 2))
    if fmt == "e4m3":
        words = by_word.astype(ml_dtypes.float8_e4m3fn).view(np.uint8)
    else:
        c = by_word.astype(ml_dtypes.float4_e2m1fn).view(np.uint8) & 0xF
        words = (c[..., 0::2] | (c[..., 1::2] << 4)).reshape(k // 512, 128, 2 * n)
    return np.ascontiguousarray(words), np.ascontiguousarray(byte.astype(np.uint8).reshape(k // 512, 16, n))


def unpack_weight(words, scales, fmt):
    g, _, n = scales.shape
    words = np.ascontiguousarray(words).reshape(g, 128, n, -1)
    if fmt == "e4m3":
        vals = words.view(ml_dtypes.float8_e4m3fn).astype(np.float64)
    else:
        nib = np.empty((g, 128, n, 4), np.uint8)
        nib[..., 0::2] = words & 0xF
        nib[..., 1::2] = words >> 4
        vals = E2M1[nib]
    vals = vals * np.repeat(np.exp2(scales.astype(np.float64) - 127.0), 8, axis=1)[..., None]
    return vals.transpose(0, 1, 3, 2).reshape(g * 512, n)


def gelu(v):
    return 0.5 * v * (1.0 + np.tanh(np.sqrt(2.0 / np.pi) * (v + 0.044715 * v**3)))


def bf(x):
    return np.asarray(x, np.float32).astype(ml_dtypes.bfloat16)


def planes(Y):
    n, m = Y.shape
    b = f64(bf(Y)).reshape(n // 32, 32, m)
    amax = np.abs(b).max(1)
    byte = np.clip(np.where(amax > 0, np.frexp(amax)[1] - 1 + 127 - 7, 1), 1, 254)
    codes = (b * np.exp2(127.0 - byte)[:, None, :]).reshape(n, m).astype(np.float32).astype(ml_dtypes.float8_e4m3fn).view(np.uint8)
    words = codes.reshape(n // 512, 128, 4, m).transpose(0, 1, 3, 2)
    return np.ascontiguousarray(words), np.ascontiguousarray(byte.astype(np.uint8).reshape(n // 512, 16, m))


K, H, N, T, S = 1024, 512, 512, 2048, 1024

def setup_inputs():
    n = np.random.standard_normal
    s = mx_kscale(K)[:, None]
    u = mx_kscale(H)[:, None]
    tab_words, tab_scales = pack_weight(n((K, T)) * s, "e4m3")
    offs = striped(np.random.permutation(T)[:S])
    w1 = (n((K, H)) / np.sqrt(K) * u.T / s).astype(np.float32)
    w2_words, w2_scales = pack_weight(n((K, H)) / np.sqrt(K) * u.T / s, "e2m1")
    w3_words, w3_scales = pack_weight(n((K, H)) / np.sqrt(K) * u.T / s, "e4m3")
    w4_words, w4_scales = pack_weight(1.5 * n((H, N)) / np.sqrt(H) / u, "e2m1")
    w5 = (n((K, N)) / np.sqrt(K) / s).astype(np.float32)
    return {"tab_words": tab_words, "tab_scales": tab_scales, "offs": offs,
            "w1": w1, "w2_words": w2_words, "w2_scales": w2_scales,
            "w3_words": w3_words, "w3_scales": w3_scales,
            "w4_words": w4_words, "w4_scales": w4_scales, "w5": w5}

def reference(tab_words, tab_scales, offs, w1, w2_words, w2_scales,
              w3_words, w3_scales, w4_words, w4_scales, w5):
    v = unpack_weight(tab_words, tab_scales, "e4m3")[:, unstriped(offs)]
    w2 = unpack_weight(w2_words, w2_scales, "e2m1")
    w3 = unpack_weight(w3_words, w3_scales, "e4m3")
    w4 = unpack_weight(w4_words, w4_scales, "e2m1")
    base = mxq(f64(w1), 0, "e4m3").T @ v
    cap = w2.T @ v
    floor_ = w3.T @ v
    h = np.maximum(np.minimum(base, cap), floor_)
    words, scales = planes(h)
    hq = mxq(h, 0, "e4m3")
    e = w4.T @ hq + mxq(f64(w5), 0, "e4m3").T @ v
    y = e / (1.0 + np.exp(-e))
    return y, h, words, scales

@@ -1,0 +1,401 @@
+from contextlib import ExitStack
+
+import concourse.mybir as mybir
+
+K, H, N, T, S = 1024, 512, 512, 2048, 1024
+FLOPS = 2 * S * (3 * K * H + H * N + K * N)
+
+F32 = mybir.dt.float32
+BF16 = mybir.dt.bfloat16
+I32 = mybir.dt.int32
+U32 = mybir.dt.uint32
+U16 = mybir.dt.uint16
+U8 = mybir.dt.uint8
+FP8X4 = mybir.dt.float8_e4m3fn_x4
+FP4X4 = mybir.dt.float4_e2m1fn_x4
+ALU = mybir.AluOpType
+ACT = mybir.ActivationFunctionType
+
+P = 128
+PASSES = 2
+HALF = 512
+CHUNK = 256
+CHUNKS = S // CHUNK
+
+
+def tile_list_margin_collar_alert_kernel(
+    tc, tab_words, tab_scales, offs, w1, w2_words, w2_scales, w3_words, w3_scales,
+    w4_words, w4_scales, w5, out_0, out_1, out_2, out_3,
+):
+    nc = tc.nc
+    with ExitStack() as ctx:
+        keep = ctx.enter_context(tc.tile_pool(name="keep", bufs=1))
+        psum = ctx.enter_context(tc.psum_pool(name="psum", bufs=1))
+
+        def sb(name, shape, dtype):
+            return keep.tile(shape, dtype, name=name, align_bytes=64)
+
+        offsets = keep.tile([P, S // 16], U16, name="offsets")
+        nc.sync.dma_start(offsets[:], offs)
+
+        banks = [psum.tile([P, 512], F32, name="bank%d" % b) for b in range(8)]
+
+        w3s_raw = sb("w3s_raw", [P, H], U8)
+        w4_s = sb("w4_s", [P, N], U8)
+        gs_low = sb("gs_low", [P, S], U8)
+        warm = sb("warm", [P, 8], F32)
+
+        early = ctx.enter_context(tc.tile_pool(name="early", bufs=1))
+        zeros = early.tile([P, 22 * 256], I32, name="zeros", offset=0)
+        tab_w = [early.tile([P, T], I32, name="tab_w%d" % a, offset=8192 * a) for a in range(PASSES)]
+        w3_raw = early.tile([P, PASSES * H], I32, name="w3_raw", offset=16384)
+        w2_raw = early.tile([P, PASSES * 2 * H], U8, name="w2_raw", offset=20480)
+        w2s_raw = early.tile([P, PASSES * H], U8, name="w2s_raw", offset=22528)
+        g_w01 = early.tile([P, HALF], U32, name="g_w01", offset=22528, align_bytes=64)
+
+        late = ctx.enter_context(tc.tile_pool(name="late", bufs=1))
+        tab_s_tile = late.tile([P, 33 * 1024], U8, name="tab_s_tile", offset=0)
+        tab_s = tab_s_tile[:, 0:T]
+        w1_raw = [late.tile([P, 4 * H], F32, name="w1_raw%d" % a, offset=8192 * a) for a in range(PASSES)]
+        w5_raw = [late.tile([P, 4 * N], F32, name="w5_raw%d" % a, offset=8192 * (2 + a)) for a in range(PASSES)]
+        w4_w = late.tile([P, 2 * N], U8, name="w4_w", offset=8192 * 4, align_bytes=64)
+
+        nc.vector.memset(tab_s.bitcast(I32), 0)
+        nc.vector.memset(zeros[:, 0:128], 0)
+        nc.vector.tensor_copy(w4_s[:].bitcast(I32), zeros[:, 0:128])
+        nc.vector.memset(w3s_raw[:].bitcast(I32), 0)
+        nc.vector.memset(w2s_raw[:].bitcast(I32), 0)
+        nc.gpsimd.memset(warm[:, 0:4], 0.0)
+        nc.gpsimd.memset(gs_low[:].bitcast(I32), 0)
+        nc.scalar.activation(warm[:, 4:8], warm[:, 0:4], ACT.Silu)
+
+        def load_words(tile, words):
+            nc.sync.dma_start(out=tile[:], in_=words.rearrange("p t i -> p (t i)").bitcast(I32))
+
+        def load_w3_scales(q):
+            nc.sync.dma_start(
+                out=w3s_raw[32 * q : 32 * q + 8, :].bitcast(I32),
+                in_=w3_scales[:, 4 * q : 4 * q + 4, :].bitcast(I32),
+            )
+
+        def load_w2_scales(q):
+            nc.sync.dma_start(
+                out=w2s_raw[32 * q : 32 * q + 4, :].bitcast(I32).rearrange("r (a c) -> r a c", a=PASSES),
+                in_=w2_scales[:, 4 * q : 4 * q + 4, :].rearrange("a r c -> r a c").bitcast(I32),
+            )
+
+        for q in range(4):
+            nc.sync.dma_start(
+                out=tab_s[32 * q : 32 * q + 8, :].bitcast(I32),
+                in_=tab_scales[:, 4 * q : 4 * q + 4, :].bitcast(I32),
+            )
+        load_words(tab_w[0], tab_words[0])
+        for q in range(4):
+            load_w3_scales(q)
+        nc.sync.dma_start(
+            out=w3_raw[:].rearrange("p (a c) -> p a c", a=PASSES),
+            in_=w3_words.rearrange("a p c i -> p a (c i)").bitcast(I32),
+        )
+        load_w2_scales(0)
+        load_w2_scales(1)
+        nc.sync.dma_start(
+            out=w2_raw[:].bitcast(I32).rearrange("p (a c) -> p a c", a=PASSES),
+            in_=w2_words.rearrange("a p c -> p a c").bitcast(I32),
+        )
+        load_w2_scales(2)
+        load_w2_scales(3)
+        load_words(tab_w[1], tab_words[1])
+        for q in range(4):
+            nc.gpsimd.dma_start(
+                out=w4_s[32 * q : 32 * q + 4, :].bitcast(I32),
+                in_=w4_scales[0, 4 * q : 4 * q + 4, :].bitcast(I32),
+            )
+
+        def load_late():
+            for a in range(PASSES):
+                nc.sync.dma_start(
+                    out=w1_raw[a][:], in_=w1[512 * a : 512 * (a + 1), :].rearrange("(p j) c -> p (j c)", j=4)
+                )
+            for a in range(PASSES):
+                nc.sync.dma_start(
+                    out=w5_raw[a][:], in_=w5[512 * a : 512 * (a + 1), :].rearrange("(p j) c -> p (j c)", j=4)
+                )
+            nc.sync.dma_start(out=w4_w[:].bitcast(I32), in_=w4_words[0].bitcast(I32))
+
+        g_w = [
+            [sb("g_w00", [P, HALF], U32), g_w01],
+            [sb("g_w10", [P, HALF], U32), sb("g_w11", [P, HALF], U32)],
+        ]
+        g_s = sb("g_s", [P, S], U8)
+
+        def half_list(h):
+            return offsets[:, 32 * h : 32 * (h + 1)]
+
+        def gather_scales():
+            nc.vector.tensor_copy(g_s[:], tab_s.indirect(offsets[:]))
+            nc.sync.dma_start(out=gs_low[0:100, :].bitcast(I32), in_=g_s[4:104, :].bitcast(I32))
+
+        def gather_words(a, h):
+            nc.vector.tensor_copy(g_w[a][h][:], tab_w[a][:].bitcast(U32).indirect(half_list(h)))
+
+        w3_s = sb("w3_s", [P, H], U8)
+        w2_s = sb("w2_s", [P, PASSES * H], U8)
+        w3_w = [sb("w3_w%d" % a, [P, H], I32) for a in range(PASSES)]
+        w2_w = [sb("w2_w%d" % a, [P, 2 * H], U8) for a in range(PASSES)]
+
+        def deal_w3_scales():
+            nc.vector.tensor_copy(
+                w3_s[:].rearrange("p (t m) -> p m t", t=4), w3s_raw[:].rearrange("p (m t) -> p m t", t=4)
+            )
+
+        def deal_w2_scales():
+            nc.vector.tensor_copy(
+                w2_s[:].rearrange("p (a t m) -> p a m t", a=PASSES, t=4),
+                w2s_raw[:].rearrange("p (a m t) -> p a m t", a=PASSES, t=4),
+            )
+
+        def deal_w3(a):
+            nc.vector.tensor_copy(
+                w3_w[a][:].rearrange("p (t m) -> p m t", t=4),
+                w3_raw[:, H * a : H * (a + 1)].rearrange("p (m t) -> p m t", t=4),
+            )
+
+        def deal_w2(a):
+            nc.vector.tensor_copy(
+                w2_w[a][:].bitcast(U16).rearrange("p (t m) -> p m t", t=4),
+                w2_raw[:, 2 * H * a : 2 * H * (a + 1)].bitcast(U16).rearrange("p (m t) -> p m t", t=4),
+            )
+
+        w1_b = [sb("w1_b%d" % a, [P, 4 * H], BF16) for a in range(PASSES)]
+        w1_w = [sb("w1_w%d" % a, [P, H], U32) for a in range(PASSES)]
+        w1_s = [sb("w1_s%d" % a, [P, H], U8) for a in range(PASSES)]
+        w5_b = [sb("w5_b%d" % a, [P, 4 * N], BF16) for a in range(PASSES)]
+        w5_w = [sb("w5_w%d" % a, [P, N], U32) for a in range(PASSES)]
+        w5_s = [sb("w5_s%d" % a, [P, N], U8) for a in range(PASSES)]
+
+        def round_w1(a):
+            nc.vector.tensor_copy(
+                w1_b[a][:].rearrange("p (t m j) -> p m j t", t=4, j=4),
+                w1_raw[a][:].rearrange("p (j m t) -> p m j t", j=4, t=4),
+            )
+
+        def quantize_w1(a):
+            nc.vector.quantize_mx(out=w1_w[a][:].bitcast(FP8X4), scales=w1_s[a][:], in_=w1_b[a][:])
+
+        def round_w5(a, u):
+            nc.scalar.copy(
+                w5_b[a][:, 1024 * u : 1024 * (u + 1)].rearrange("p (c i j) -> p c j i", i=4, j=4),
+                w5_raw[a][:].rearrange("p (j c i) -> p c j i", j=4, i=4)[:, 64 * u : 64 * (u + 1), :, :],
+            )
+
+        def quantize_w5(a, u):
+            nc.vector.quantize_mx(
+                out=w5_w[a][:, 256 * u : 256 * (u + 1)].bitcast(FP8X4),
+                scales=w5_s[a][:, 256 * u : 256 * (u + 1)],
+                in_=w5_b[a][:, 1024 * u : 1024 * (u + 1)],
+            )
+
+        def table(a, c):
+            h, lo = c // 2, CHUNK * (c % 2)
+            return g_w[a][h][:, lo : lo + CHUNK].bitcast(FP8X4), g_s[4 * a : P, CHUNK * c : CHUNK * (c + 1)]
+
+        def cap_pass(a, h, t, bank):
+            plane = g_s if a == 0 else gs_low
+            nc.tensor.matmul_mx(
+                out=bank[:],
+                lhsT=w2_w[a][:, 256 * t : 256 * (t + 1)].bitcast(FP4X4),
+                lhsT_scale=w2_s[:, H * a + P * t : H * a + P * (t + 1)],
+                rhs=g_w[a][h][:].bitcast(FP8X4),
+                rhs_scale=plane[:, HALF * h : HALF * (h + 1)],
+                start=(a == 0),
+                stop=(a == PASSES - 1),
+            )
+
+        def chunk_pass(words, scales, a, c, u, bank, first, last):
+            rhs, rhs_scale = table(a, c)
+            for s in range(2):
+                cols = slice(P * (2 * u + s), P * (2 * u + s + 1))
+                nc.tensor.matmul_mx(
+                    out=bank[:, CHUNK * s : CHUNK * (s + 1)],
+                    lhsT=words[:, cols].bitcast(FP8X4),
+                    lhsT_scale=scales[:, cols],
+                    rhs=rhs,
+                    rhs_scale=rhs_scale,
+                    start=(first and s == 0),
+                    stop=(last and s == 1),
+                )
+
+        def floor_pass(a, c, u, bank):
+            chunk_pass(w3_w[a], w3_s[4 * a : P, :], a, c, u, bank, a == 0, a == PASSES - 1)
+
+        def base_pass(a, c, u, bank):
+            chunk_pass(w1_w[a], w1_s[a], a, c, u, bank, a == 0, a == PASSES - 1)
+
+        cap = [[sb("cap%d_%d" % (h, u), [P, 2, HALF], F32) for u in range(2)] for h in range(2)]
+        low = [[sb("low%d_%d" % (c, u), [P, 2 * CHUNK], F32) for u in range(2)] for c in range(CHUNKS)]
+        hf = [sb("hf%d" % c, [P, 4 * CHUNK], F32) for c in range(CHUNKS)]
+        hb = [sb("hb%d" % c, [P, 4 * CHUNK], BF16) for c in range(CHUNKS)]
+        h_w = sb("h_w", [P, S], U32)
+        h_s = sb("h_s", [P, S], U8)
+        y = [[sb("y%d_%d" % (c, u), [P, 2 * CHUNK], F32) for u in range(2)] for c in range(CHUNKS)]
+        h_rows = out_1.rearrange("(p t) j -> p t j", t=4)
+        y_rows = out_0.rearrange("(u p) j -> p u j", p=P)
+
+        def save_cap(h, t, bank):
+            nc.scalar.copy(cap[h][t // 2][:, t % 2, :], bank[:])
+
+        def take_min(c, u, bank):
+            lo = CHUNK * (c % 2)
+            nc.vector.tensor_tensor(
+                low[c][u][:].rearrange("p (s j) -> p s j", s=2),
+                bank[:].rearrange("p (s j) -> p s j", s=2),
+                cap[c // 2][u][:, :, lo : lo + CHUNK],
+                ALU.min,
+            )
+
+        def take_max(c, u, bank):
+            nc.vector.tensor_tensor(hf[c][:, 512 * u : 512 * (u + 1)], bank[:], low[c][u][:], ALU.max)
+
+        def store_h(c):
+            nc.sync.dma_start(
+                out=h_rows[:, :, CHUNK * c : CHUNK * (c + 1)], in_=hf[c][:].rearrange("p (t j) -> p t j", t=4)
+            )
+
+        def round_h(c):
+            copy = nc.vector.tensor_copy if c == CHUNKS - 1 else nc.scalar.copy
+            copy(
+                hb[c][:].rearrange("p (c i t) -> p c t i", i=4, t=4),
+                hf[c][:].rearrange("p (t c i) -> p c t i", t=4, i=4),
+            )
+
+        def quantize_h(c):
+            cols = slice(CHUNK * c, CHUNK * (c + 1))
+            nc.vector.quantize_mx(out=h_w[:, cols].bitcast(FP8X4), scales=h_s[:, cols], in_=hb[c][:])
+
+        def direct_passes(c, u, bank):
+            for a in range(PASSES):
+                chunk_pass(w5_w[a], w5_s[a], a, c, u, bank, a == 0, False)
+
+        def collar_passes(c, u, bank):
+            for s in range(2):
+                n = 2 * u + s
+                for k in range(2):
+                    cols = slice(CHUNK * c + P * k, CHUNK * c + P * (k + 1))
+                    nc.tensor.matmul_mx(
+                        out=bank[:, CHUNK * s + P * k : CHUNK * s + P * (k + 1)],
+                        lhsT=w4_w[:, 256 * n : 256 * (n + 1)].bitcast(FP4X4),
+                        lhsT_scale=w4_s[:, P * n : P * (n + 1)],
+                        rhs=h_w[:, cols].bitcast(FP8X4),
+                        rhs_scale=h_s[:, cols],
+                        start=False,
+                        stop=(s == 1 and k == 1),
+                    )
+
+        def finish(c, u, bank):
+            nc.scalar.activation(y[c][u][:], bank[:], ACT.Silu)
+            nc.sync.dma_start(
+                out=y_rows[:, 2 * u : 2 * u + 2, CHUNK * c : CHUNK * (c + 1)],
+                in_=y[c][u][:].rearrange("p (s j) -> p s j", s=2),
+            )
+
+        gather_scales()
+        load_late()
+        gather_words(0, 0)
+        deal_w3_scales()
+        deal_w3(0)
+        for c in range(2):
+            for u in range(2):
+                floor_pass(0, c, u, banks[4 + 2 * c + u])
+        deal_w2(0)
+        deal_w2_scales()
+        for t in range(4):
+            cap_pass(0, 0, t, banks[t])
+        deal_w2(1)
+        deal_w3(1)
+        gather_words(1, 0)
+        for t in range(4):
+            cap_pass(1, 0, t, banks[t])
+            save_cap(0, t, banks[t])
+        for c in range(2):
+            for u in range(2):
+                floor_pass(1, c, u, banks[4 + 2 * c + u])
+        gather_words(0, 1)
+        gather_words(1, 1)
+        for t in range(4):
+            for a in range(PASSES):
+                cap_pass(a, 1, t, banks[t])
+            save_cap(1, t, banks[t])
+        round_w1(0)
+        quantize_w1(0)
+        round_w1(1)
+        quantize_w1(1)
+
+        def base(c, pair):
+            for u in range(2):
+                for a in range(PASSES):
+                    base_pass(a, c, u, pair[u])
+
+        def floor_(c, pair):
+            for u in range(2):
+                for a in range(PASSES):
+                    floor_pass(a, c, u, pair[u])
+
+        def collar(c, base_pair, floor_pair):
+            for u in range(2):
+                take_min(c, u, base_pair[u])
+            for u in range(2):
+                take_max(c, u, floor_pair[u])
+            store_h(c)
+            round_h(c)
+
+        def direct(c, pair):
+            for u in range(2):
+                direct_passes(c, u, pair[u])
+
+        def second(c, pair):
+            for u in range(2):
+                collar_passes(c, u, pair[u])
+                finish(c, u, pair[u])
+
+        def store_words(h):
+            cols = slice(HALF * h, HALF * (h + 1))
+            nc.sync.dma_start(
+                out=out_2[0].rearrange("p m t -> p (m t)").bitcast(I32)[:, cols], in_=h_w[:, cols].bitcast(I32)
+            )
+
+        pa, pb, pc, pd = banks[0:2], banks[2:4], banks[4:6], banks[6:8]
+        base(0, pa)
+        base(1, pb)
+        for u in range(2):
+            round_w5(0, u)
+        collar(0, pa, pc)
+        for u in range(2):
+            round_w5(1, u)
+        base(2, pa)
+        floor_(2, pc)
+        collar(1, pb, pd)
+        quantize_h(0)
+        for u in range(2):
+            for a in range(PASSES):
+                quantize_w5(a, u)
+        base(3, pb)
+        direct(0, pd)
+        second(0, pd)
+        collar(2, pa, pc)
+        quantize_h(1)
+        store_words(0)
+        floor_(3, pa)
+        direct(1, pc)
+        second(1, pc)
+        direct(3, pd)
+        collar(3, pb, pa)
+        quantize_h(2)
+        direct(2, pb)
+        second(2, pb)
+        quantize_h(3)
+        second(3, pd)
+        store_words(1)
+        for q in range(4):
+            nc.scalar.dma_start(
+                out=out_3[0, 4 * q : 4 * q + 4, :].bitcast(I32), in_=h_s[32 * q : 32 * q + 4, :].bitcast(I32)
+            )

@@ -40,49 +40,41 @@ def tile_list_margin_collar_alert_kernel(
 
         banks = [psum.tile([P, 512], F32, name="bank%d" % b) for b in range(8)]
 
-        w3s_raw = sb("w3s_raw", [P, H], U8)
-        w4_s = sb("w4_s", [P, N], U8)
         gs_low = sb("gs_low", [P, S], U8)
         warm = sb("warm", [P, 8], F32)
 
-        early = ctx.enter_context(tc.tile_pool(name="early", bufs=1))
-        zeros = early.tile([P, 22 * 256], I32, name="zeros", offset=0)
-        tab_w = [early.tile([P, T], I32, name="tab_w%d" % a, offset=8192 * a) for a in range(PASSES)]
-        w3_raw = early.tile([P, PASSES * H], I32, name="w3_raw", offset=16384)
-        w2_raw = early.tile([P, PASSES * 2 * H], U8, name="w2_raw", offset=20480)
-        w2s_raw = early.tile([P, PASSES * H], U8, name="w2s_raw", offset=22528)
-        g_w01 = early.tile([P, HALF], U32, name="g_w01", offset=22528, align_bytes=64)
+        stage = ctx.enter_context(tc.tile_pool(name="stage", bufs=1))
 
-        late = ctx.enter_context(tc.tile_pool(name="late", bufs=1))
-        tab_s_tile = late.tile([P, 33 * 1024], U8, name="tab_s_tile", offset=0)
+        def staged(name, shape, dtype, kib):
+            return stage.tile(shape, dtype, name=name, offset=1024 * kib, align_bytes=64)
+
+        zeros_a = staged("zeros_a", [P, 12 * 256], I32, 0)
+        zeros_b = staged("zeros_b", [P, 10 * 256], I32, 13)
+        tab_w = [staged("tab_w0", [P, T], I32, 0), staged("tab_w1", [P, T], I32, 13)]
+        w3_raw = staged("w3_raw", [P, PASSES * H], I32, 8)
+        w3s_raw = staged("w3s_raw", [P, H], U8, 12)
+        g_w01 = staged("g_w01", [P, HALF], U32, 11)
+        w2_raw = staged("w2_raw", [P, PASSES * 2 * H], U8, 21)
+        w2s_raw = staged("w2s_raw", [P, PASSES * H], U8, 23)
+        g_w11 = staged("g_w11", [P, HALF], U32, 22)
+        tab_s_tile = staged("tab_s_tile", [P, 34 * 1024], U8, 24)
         tab_s = tab_s_tile[:, 0:T]
-        w1_raw = [late.tile([P, 4 * H], F32, name="w1_raw%d" % a, offset=8192 * a) for a in range(PASSES)]
-        w5_raw = [late.tile([P, 4 * N], F32, name="w5_raw%d" % a, offset=8192 * (2 + a)) for a in range(PASSES)]
-        w4_w = late.tile([P, 2 * N], U8, name="w4_w", offset=8192 * 4, align_bytes=64)
+        w1_raw = [staged("w1_raw%d" % a, [P, 4 * H], F32, 24 + 8 * a) for a in range(PASSES)]
+        w5_raw = [staged("w5_raw%d" % a, [P, 4 * N], F32, 40 + 8 * a) for a in range(PASSES)]
+        w4_w = staged("w4_w", [P, 2 * N], U8, 56)
+        w4_s = staged("w4_s", [P, N], U8, 57)
 
         nc.vector.memset(tab_s.bitcast(I32), 0)
-        nc.vector.memset(zeros[:, 0:128], 0)
-        nc.vector.tensor_copy(w4_s[:].bitcast(I32), zeros[:, 0:128])
-        nc.vector.memset(w3s_raw[:].bitcast(I32), 0)
-        nc.vector.memset(w2s_raw[:].bitcast(I32), 0)
-        nc.gpsimd.memset(warm[:, 0:4], 0.0)
+        nc.vector.memset(zeros_a[:, 0:128], 0)
+        nc.vector.tensor_copy(w3s_raw[:].bitcast(I32), zeros_a[:, 0:128])
+        nc.vector.memset(zeros_b[:, 0:256], 0)
+        nc.vector.tensor_copy(w2s_raw[:].bitcast(I32), zeros_b[:, 0:256])
         nc.gpsimd.memset(gs_low[:].bitcast(I32), 0)
+        nc.gpsimd.memset(warm[:, 0:4], 0.0)
         nc.scalar.activation(warm[:, 4:8], warm[:, 0:4], ACT.Silu)
 
         def load_words(tile, words):
             nc.sync.dma_start(out=tile[:], in_=words.rearrange("p t i -> p (t i)").bitcast(I32))
-
-        def load_w3_scales(q):
-            nc.sync.dma_start(
-                out=w3s_raw[32 * q : 32 * q + 8, :].bitcast(I32),
-                in_=w3_scales[:, 4 * q : 4 * q + 4, :].bitcast(I32),
-            )
-
-        def load_w2_scales(q):
-            nc.sync.dma_start(
-                out=w2s_raw[32 * q : 32 * q + 4, :].bitcast(I32).rearrange("r (a c) -> r a c", a=PASSES),
-                in_=w2_scales[:, 4 * q : 4 * q + 4, :].rearrange("a r c -> r a c").bitcast(I32),
-            )
 
         for q in range(4):
             nc.sync.dma_start(
@@ -90,25 +82,24 @@ def tile_list_margin_collar_alert_kernel(
                 in_=tab_scales[:, 4 * q : 4 * q + 4, :].bitcast(I32),
             )
         load_words(tab_w[0], tab_words[0])
-        for q in range(4):
-            load_w3_scales(q)
         nc.sync.dma_start(
             out=w3_raw[:].rearrange("p (a c) -> p a c", a=PASSES),
             in_=w3_words.rearrange("a p c i -> p a (c i)").bitcast(I32),
         )
-        load_w2_scales(0)
-        load_w2_scales(1)
+        for q in range(4):
+            nc.sync.dma_start(
+                out=w3s_raw[32 * q : 32 * q + 8, :].bitcast(I32),
+                in_=w3_scales[:, 4 * q : 4 * q + 4, :].bitcast(I32),
+            )
+        load_words(tab_w[1], tab_words[1])
         nc.sync.dma_start(
             out=w2_raw[:].bitcast(I32).rearrange("p (a c) -> p a c", a=PASSES),
             in_=w2_words.rearrange("a p c -> p a c").bitcast(I32),
         )
-        load_w2_scales(2)
-        load_w2_scales(3)
-        load_words(tab_w[1], tab_words[1])
         for q in range(4):
-            nc.gpsimd.dma_start(
-                out=w4_s[32 * q : 32 * q + 4, :].bitcast(I32),
-                in_=w4_scales[0, 4 * q : 4 * q + 4, :].bitcast(I32),
+            nc.sync.dma_start(
+                out=w2s_raw[32 * q : 32 * q + 4, :].bitcast(I32).rearrange("r (a c) -> r a c", a=PASSES),
+                in_=w2_scales[:, 4 * q : 4 * q + 4, :].rearrange("a r c -> r a c").bitcast(I32),
             )
 
         def load_late():
@@ -121,10 +112,16 @@ def tile_list_margin_collar_alert_kernel(
                     out=w5_raw[a][:], in_=w5[512 * a : 512 * (a + 1), :].rearrange("(p j) c -> p (j c)", j=4)
                 )
             nc.sync.dma_start(out=w4_w[:].bitcast(I32), in_=w4_words[0].bitcast(I32))
+            nc.gpsimd.memset(w4_s[:].bitcast(I32), 0)
+            for q in range(4):
+                nc.sync.dma_start(
+                    out=w4_s[32 * q : 32 * q + 4, :].bitcast(I32),
+                    in_=w4_scales[0, 4 * q : 4 * q + 4, :].bitcast(I32),
+                )
 
         g_w = [
             [sb("g_w00", [P, HALF], U32), g_w01],
-            [sb("g_w10", [P, HALF], U32), sb("g_w11", [P, HALF], U32)],
+            [sb("g_w10", [P, HALF], U32), g_w11],
         ]
         g_s = sb("g_s", [P, S], U8)
 
@@ -306,29 +303,24 @@ def tile_list_margin_collar_alert_kernel(
         for c in range(2):
             for u in range(2):
                 floor_pass(0, c, u, banks[4 + 2 * c + u])
-        deal_w2(0)
-        deal_w2_scales()
-        for t in range(4):
-            cap_pass(0, 0, t, banks[t])
-        deal_w2(1)
         deal_w3(1)
         gather_words(1, 0)
-        for t in range(4):
-            cap_pass(1, 0, t, banks[t])
-            save_cap(0, t, banks[t])
         for c in range(2):
             for u in range(2):
                 floor_pass(1, c, u, banks[4 + 2 * c + u])
+        deal_w2(0)
+        deal_w2_scales()
+        deal_w2(1)
         gather_words(0, 1)
         gather_words(1, 1)
-        for t in range(4):
-            for a in range(PASSES):
-                cap_pass(a, 1, t, banks[t])
-            save_cap(1, t, banks[t])
-        round_w1(0)
-        quantize_w1(0)
-        round_w1(1)
-        quantize_w1(1)
+        for h in range(2):
+            for t in range(4):
+                for a in range(PASSES):
+                    cap_pass(a, h, t, banks[t])
+                save_cap(h, t, banks[t])
+        for a in range(PASSES):
+            round_w1(a)
+            quantize_w1(a)
 
         def base(c, pair):
             for u in range(2):
@@ -364,8 +356,10 @@ def tile_list_margin_collar_alert_kernel(
             )
 
         pa, pb, pc, pd = banks[0:2], banks[2:4], banks[4:6], banks[6:8]
-        base(0, pa)
-        base(1, pb)
+        for c in range(2):
+            for a in range(PASSES):
+                for u in range(2):
+                    base_pass(a, c, u, banks[2 * c + u])
         for u in range(2):
             round_w5(0, u)
         collar(0, pa, pc)
@@ -387,15 +381,20 @@ def tile_list_margin_collar_alert_kernel(
         floor_(3, pa)
         direct(1, pc)
         second(1, pc)
-        direct(3, pd)
-        collar(3, pb, pa)
+        direct(2, pd)
+        for u in range(2):
+            take_min(3, u, pb[u])
         quantize_h(2)
-        direct(2, pb)
-        second(2, pb)
+        second(2, pd)
+        direct(3, pb)
+        for u in range(2):
+            take_max(3, u, pa[u])
+        store_h(3)
+        round_h(3)
         quantize_h(3)
-        second(3, pd)
+        second(3, pb)
         store_words(1)
         for q in range(4):
-            nc.scalar.dma_start(
+            nc.sync.dma_start(
                 out=out_3[0, 4 * q : 4 * q + 4, :].bitcast(I32), in_=h_s[32 * q : 32 * q + 4, :].bitcast(I32)
             )

@@ -19,8 +19,9 @@ ACT = mybir.ActivationFunctionType
 P = 128
 PASSES = 2
 HALF = 512
-CHUNK = 256
-CHUNKS = S // CHUNK
+BANK = 512
+WIDTHS = (256, 256, 256, 128, 128)
+STARTS = tuple(sum(WIDTHS[:c]) for c in range(len(WIDTHS)))
 
 
 def tile_list_margin_collar_alert_kernel(
@@ -38,50 +39,68 @@ def tile_list_margin_collar_alert_kernel(
         offsets = keep.tile([P, S // 16], U16, name="offsets")
         nc.sync.dma_start(offsets[:], offs)
 
-        banks = [psum.tile([P, 512], F32, name="bank%d" % b) for b in range(8)]
-
+        banks = [psum.tile([P, BANK], F32, name="bank%d" % b) for b in range(8)]
+        g_s = sb("g_s", [P, S], U8)
         gs_low = sb("gs_low", [P, S], U8)
         warm = sb("warm", [P, 8], F32)
 
         stage = ctx.enter_context(tc.tile_pool(name="stage", bufs=1))
 
-        def staged(name, shape, dtype, kib):
-            return stage.tile(shape, dtype, name=name, offset=1024 * kib, align_bytes=64)
+        def staged(name, shape, dtype, at):
+            return stage.tile(shape, dtype, name=name, offset=at, align_bytes=64)
 
-        zeros_a = staged("zeros_a", [P, 12 * 256], I32, 0)
-        zeros_b = staged("zeros_b", [P, 10 * 256], I32, 13)
-        tab_w = [staged("tab_w0", [P, T], I32, 0), staged("tab_w1", [P, T], I32, 13)]
-        w3_raw = staged("w3_raw", [P, PASSES * H], I32, 8)
-        w3s_raw = staged("w3s_raw", [P, H], U8, 12)
-        g_w01 = staged("g_w01", [P, HALF], U32, 11)
-        w2_raw = staged("w2_raw", [P, PASSES * 2 * H], U8, 21)
-        w2s_raw = staged("w2s_raw", [P, PASSES * H], U8, 23)
-        g_w11 = staged("g_w11", [P, HALF], U32, 22)
-        tab_s_tile = staged("tab_s_tile", [P, 34 * 1024], U8, 24)
-        tab_s = tab_s_tile[:, 0:T]
-        w1_raw = [staged("w1_raw%d" % a, [P, 4 * H], F32, 24 + 8 * a) for a in range(PASSES)]
-        w5_raw = [staged("w5_raw%d" % a, [P, 4 * N], F32, 40 + 8 * a) for a in range(PASSES)]
-        w4_w = staged("w4_w", [P, 2 * N], U8, 56)
-        w4_s = staged("w4_s", [P, N], U8, 57)
+        KB = 1024
+        tab_s = staged("tab_s", [P, T], U8, 0)
+        zeros_a = staged("zeros_a", [P, 256], I32, 11 * KB)
+        zeros_b = staged("zeros_b", [P, 256], I32, 26 * KB - 512)
+        zeros_c = staged("zeros_c", [P, 128], I32, 34 * KB)
+        tab_w = [staged("tab_w0", [P, T], I32, 4 * KB), staged("tab_w1", [P, T], I32, 26 * KB)]
+        w2_raw = staged("w2_raw", [P, PASSES * 2 * H], U8, 13 * KB)
+        w3_raw = staged("w3_raw", [P, PASSES * H], I32, 34 * KB)
+        w2s_raw = staged("w2s_raw", [P, PASSES * H], U8, 38 * KB)
+        w3s_raw = staged("w3s_raw", [P, H], U8, 40 * KB)
+        g_w01 = staged("g_w01", [P, HALF], U32, 38 * KB)
+        w1_early = staged("w1_early", [P, 2 * H], F32, 22 * KB)
+        w1_late = staged("w1_late", [P, 2 * H], F32, 0)
+        w1_raw1 = staged("w1_raw1", [P, 4 * H], F32, 14 * KB)
+        w5_raw = [staged("w5_raw0", [P, 4 * N], F32, 4 * KB), staged("w5_raw1", [P, 4 * N], F32, 26 * KB)]
+        w4_w = staged("w4_w", [P, 2 * N], U8, 34 * KB)
+        w4_s = staged("w4_s", [P, N], U8, 40 * KB)
 
-        nc.vector.memset(tab_s.bitcast(I32), 0)
-        nc.vector.memset(zeros_a[:, 0:128], 0)
-        nc.vector.tensor_copy(w3s_raw[:].bitcast(I32), zeros_a[:, 0:128])
-        nc.vector.memset(zeros_b[:, 0:256], 0)
-        nc.vector.tensor_copy(w2s_raw[:].bitcast(I32), zeros_b[:, 0:256])
-        nc.gpsimd.memset(gs_low[:].bitcast(I32), 0)
+        nc.gpsimd.memset(tab_s[:].bitcast(I32), 0)
+        nc.vector.memset(zeros_a[:], 0)
+        nc.vector.tensor_copy(w2s_raw[:].bitcast(I32), zeros_a[:])
+        nc.vector.memset(zeros_b[:], 0)
+        nc.vector.memset(zeros_c[:], 0)
+        nc.vector.tensor_copy(gs_low[:].bitcast(I32), zeros_b[:])
+        nc.vector.tensor_copy(w3s_raw[:].bitcast(I32), zeros_c[:])
         nc.gpsimd.memset(warm[:, 0:4], 0.0)
         nc.scalar.activation(warm[:, 4:8], warm[:, 0:4], ACT.Silu)
 
         def load_words(tile, words):
             nc.sync.dma_start(out=tile[:], in_=words.rearrange("p t i -> p (t i)").bitcast(I32))
 
+        def load_rows(tile, w, a):
+            nc.sync.dma_start(
+                out=tile[:], in_=w[512 * a : 512 * (a + 1), :].rearrange("(p j) c -> p (j c)", j=4)
+            )
+
+        nc.sync.dma_start(
+            out=w2_raw[:].bitcast(I32).rearrange("p (a c) -> p a c", a=PASSES),
+            in_=w2_words.rearrange("a p c -> p a c").bitcast(I32),
+        )
+        ts_rows = tab_scales.rearrange("a (q r) t -> r q a t", r=4)
+        for r in range(4):
+            nc.sync.dma_start(out=tab_s[r:P:16, :].bitcast(I32), in_=ts_rows[r].bitcast(I32))
+        load_words(tab_w[0], tab_words[0])
         for q in range(4):
             nc.sync.dma_start(
-                out=tab_s[32 * q : 32 * q + 8, :].bitcast(I32),
-                in_=tab_scales[:, 4 * q : 4 * q + 4, :].bitcast(I32),
+                out=w2s_raw[32 * q : 32 * q + 4, :].bitcast(I32).rearrange("r (a c) -> r a c", a=PASSES),
+                in_=w2_scales[:, 4 * q : 4 * q + 4, :].rearrange("a r c -> r a c").bitcast(I32),
             )
-        load_words(tab_w[0], tab_words[0])
+        w1_first = w1[0:512, :].rearrange("(p j) c -> p j c", j=4)
+        nc.sync.dma_start(out=w1_early[:].rearrange("p (j c) -> p j c", j=4), in_=w1_first[:, :, 0:256])
+        load_words(tab_w[1], tab_words[1])
         nc.sync.dma_start(
             out=w3_raw[:].rearrange("p (a c) -> p a c", a=PASSES),
             in_=w3_words.rearrange("a p c i -> p a (c i)").bitcast(I32),
@@ -91,263 +110,176 @@ def tile_list_margin_collar_alert_kernel(
                 out=w3s_raw[32 * q : 32 * q + 8, :].bitcast(I32),
                 in_=w3_scales[:, 4 * q : 4 * q + 4, :].bitcast(I32),
             )
-        load_words(tab_w[1], tab_words[1])
-        nc.sync.dma_start(
-            out=w2_raw[:].bitcast(I32).rearrange("p (a c) -> p a c", a=PASSES),
-            in_=w2_words.rearrange("a p c -> p a c").bitcast(I32),
-        )
-        for q in range(4):
-            nc.sync.dma_start(
-                out=w2s_raw[32 * q : 32 * q + 4, :].bitcast(I32).rearrange("r (a c) -> r a c", a=PASSES),
-                in_=w2_scales[:, 4 * q : 4 * q + 4, :].rearrange("a r c -> r a c").bitcast(I32),
-            )
-
-        def load_late():
-            for a in range(PASSES):
-                nc.sync.dma_start(
-                    out=w1_raw[a][:], in_=w1[512 * a : 512 * (a + 1), :].rearrange("(p j) c -> p (j c)", j=4)
-                )
-            for a in range(PASSES):
-                nc.sync.dma_start(
-                    out=w5_raw[a][:], in_=w5[512 * a : 512 * (a + 1), :].rearrange("(p j) c -> p (j c)", j=4)
-                )
-            nc.sync.dma_start(out=w4_w[:].bitcast(I32), in_=w4_words[0].bitcast(I32))
-            nc.gpsimd.memset(w4_s[:].bitcast(I32), 0)
-            for q in range(4):
-                nc.sync.dma_start(
-                    out=w4_s[32 * q : 32 * q + 4, :].bitcast(I32),
-                    in_=w4_scales[0, 4 * q : 4 * q + 4, :].bitcast(I32),
-                )
 
         g_w = [
             [sb("g_w00", [P, HALF], U32), g_w01],
-            [sb("g_w10", [P, HALF], U32), g_w11],
+            [sb("g_w10", [P, HALF], U32), sb("g_w11", [P, HALF], U32)],
         ]
-        g_s = sb("g_s", [P, S], U8)
-
-        def half_list(h):
-            return offsets[:, 32 * h : 32 * (h + 1)]
-
-        def gather_scales():
-            nc.vector.tensor_copy(g_s[:], tab_s.indirect(offsets[:]))
-            nc.sync.dma_start(out=gs_low[0:100, :].bitcast(I32), in_=g_s[4:104, :].bitcast(I32))
+        planes = [g_s, gs_low]
 
         def gather_words(a, h):
-            nc.vector.tensor_copy(g_w[a][h][:], tab_w[a][:].bitcast(U32).indirect(half_list(h)))
+            nc.vector.tensor_copy(
+                g_w[a][h][:], tab_w[a][:].bitcast(U32).indirect(offsets[:, 32 * h : 32 * (h + 1)])
+            )
 
         w3_s = sb("w3_s", [P, H], U8)
-        w2_s = sb("w2_s", [P, PASSES * H], U8)
+        ws = [sb("ws%d" % a, [P, H], U8) for a in range(PASSES)]
         w3_w = [sb("w3_w%d" % a, [P, H], I32) for a in range(PASSES)]
         w2_w = [sb("w2_w%d" % a, [P, 2 * H], U8) for a in range(PASSES)]
 
-        def deal_w3_scales():
+        def deal(dst, src):
             nc.vector.tensor_copy(
-                w3_s[:].rearrange("p (t m) -> p m t", t=4), w3s_raw[:].rearrange("p (m t) -> p m t", t=4)
+                dst.rearrange("p (a t m) -> p a m t", t=4, m=P), src.rearrange("p (a m t) -> p a m t", t=4, m=P)
             )
 
-        def deal_w2_scales():
-            nc.vector.tensor_copy(
-                w2_s[:].rearrange("p (a t m) -> p a m t", a=PASSES, t=4),
-                w2s_raw[:].rearrange("p (a m t) -> p a m t", a=PASSES, t=4),
-            )
-
-        def deal_w3(a):
-            nc.vector.tensor_copy(
-                w3_w[a][:].rearrange("p (t m) -> p m t", t=4),
-                w3_raw[:, H * a : H * (a + 1)].rearrange("p (m t) -> p m t", t=4),
-            )
-
-        def deal_w2(a):
-            nc.vector.tensor_copy(
-                w2_w[a][:].bitcast(U16).rearrange("p (t m) -> p m t", t=4),
-                w2_raw[:, 2 * H * a : 2 * H * (a + 1)].bitcast(U16).rearrange("p (m t) -> p m t", t=4),
-            )
-
-        w1_b = [sb("w1_b%d" % a, [P, 4 * H], BF16) for a in range(PASSES)]
+        w1_b0 = sb("w1_b0", [P, 4 * H], BF16)
+        w1_b = [[w1_b0[:, 0 : 2 * H], w1_b0[:, 2 * H : 4 * H]]]
+        w1_b.append([sb("w1_b1_%d" % u, [P, 2 * H], BF16) for u in range(2)])
         w1_w = [sb("w1_w%d" % a, [P, H], U32) for a in range(PASSES)]
         w1_s = [sb("w1_s%d" % a, [P, H], U8) for a in range(PASSES)]
-        w5_b = [sb("w5_b%d" % a, [P, 4 * N], BF16) for a in range(PASSES)]
+        w5_b = [[sb("w5_b%d_%d" % (a, u), [P, 2 * N], BF16) for u in range(2)] for a in range(PASSES)]
         w5_w = [sb("w5_w%d" % a, [P, N], U32) for a in range(PASSES)]
         w5_s = [sb("w5_s%d" % a, [P, N], U8) for a in range(PASSES)]
 
-        def round_w1(a):
-            nc.vector.tensor_copy(
-                w1_b[a][:].rearrange("p (t m j) -> p m j t", t=4, j=4),
-                w1_raw[a][:].rearrange("p (j m t) -> p m j t", j=4, t=4),
+        def round_w1_first(copy, raw, v):
+            copy(
+                w1_b0[:].rearrange("p (t m j) -> p m j t", t=4, j=4)[:, 64 * v : 64 * (v + 1), :, :],
+                raw[:].rearrange("p (j m t) -> p m j t", j=4, t=4),
             )
 
-        def quantize_w1(a):
-            nc.vector.quantize_mx(out=w1_w[a][:].bitcast(FP8X4), scales=w1_s[a][:], in_=w1_b[a][:])
+        def round_w1_second(u):
+            nc.vector.tensor_copy(
+                w1_b[1][u][:].rearrange("p (t m j) -> p m j t", t=2, j=4),
+                w1_raw1[:].rearrange("p (j m t) -> p m j t", j=4, t=4)[:, :, :, 2 * u : 2 * u + 2],
+            )
 
         def round_w5(a, u):
             nc.scalar.copy(
-                w5_b[a][:, 1024 * u : 1024 * (u + 1)].rearrange("p (c i j) -> p c j i", i=4, j=4),
+                w5_b[a][u][:].rearrange("p (c i j) -> p c j i", i=4, j=4),
                 w5_raw[a][:].rearrange("p (j c i) -> p c j i", j=4, i=4)[:, 64 * u : 64 * (u + 1), :, :],
             )
 
-        def quantize_w5(a, u):
+        def round_w5_pool(a, u):
+            for v in range(2):
+                lo = 256 * u + 128 * v
+                nc.gpsimd.tensor_scalar(
+                    w5_b[a][u][:, 512 * v : 512 * (v + 1)].rearrange("p (c j) -> p c j", j=4),
+                    w5_raw[a][:].rearrange("p (j c) -> p c j", j=4)[:, lo : lo + 128, :],
+                    1.0, 0.0, ALU.mult, ALU.add,
+                )
+
+        def quantize_w(words, scales, rounded, a, u):
+            cols = slice(256 * u, 256 * (u + 1))
             nc.vector.quantize_mx(
-                out=w5_w[a][:, 256 * u : 256 * (u + 1)].bitcast(FP8X4),
-                scales=w5_s[a][:, 256 * u : 256 * (u + 1)],
-                in_=w5_b[a][:, 1024 * u : 1024 * (u + 1)],
+                out=words[a][:, cols].bitcast(FP8X4), scales=scales[a][:, cols], in_=rounded[a][u][:]
             )
 
-        def table(a, c):
-            h, lo = c // 2, CHUNK * (c % 2)
-            return g_w[a][h][:, lo : lo + CHUNK].bitcast(FP8X4), g_s[4 * a : P, CHUNK * c : CHUNK * (c + 1)]
-
-        def cap_pass(a, h, t, bank):
-            plane = g_s if a == 0 else gs_low
+        def cap_pass(a, h, t):
             nc.tensor.matmul_mx(
-                out=bank[:],
+                out=banks[4 * h + t][:],
                 lhsT=w2_w[a][:, 256 * t : 256 * (t + 1)].bitcast(FP4X4),
-                lhsT_scale=w2_s[:, H * a + P * t : H * a + P * (t + 1)],
+                lhsT_scale=ws[a][:, P * t : P * (t + 1)],
                 rhs=g_w[a][h][:].bitcast(FP8X4),
-                rhs_scale=plane[:, HALF * h : HALF * (h + 1)],
+                rhs_scale=planes[a][:, HALF * h : HALF * (h + 1)],
                 start=(a == 0),
                 stop=(a == PASSES - 1),
             )
 
-        def chunk_pass(words, scales, a, c, u, bank, first, last):
-            rhs, rhs_scale = table(a, c)
-            for s in range(2):
-                cols = slice(P * (2 * u + s), P * (2 * u + s + 1))
-                nc.tensor.matmul_mx(
-                    out=bank[:, CHUNK * s : CHUNK * (s + 1)],
-                    lhsT=words[:, cols].bitcast(FP8X4),
-                    lhsT_scale=scales[:, cols],
-                    rhs=rhs,
-                    rhs_scale=rhs_scale,
-                    start=(first and s == 0),
-                    stop=(last and s == 1),
-                )
+        def tiles_of(c, u):
+            per_bank = BANK // WIDTHS[c]
+            return range(per_bank * u, per_bank * (u + 1))
 
-        def floor_pass(a, c, u, bank):
-            chunk_pass(w3_w[a], w3_s[4 * a : P, :], a, c, u, bank, a == 0, a == PASSES - 1)
+        def table_passes(words, scales, c, u, bank, closes):
+            width, lo = WIDTHS[c], STARTS[c] % HALF
+            tiles = tiles_of(c, u)
+            for a in range(PASSES):
+                for s, t in enumerate(tiles):
+                    cols = slice(P * t, P * (t + 1))
+                    nc.tensor.matmul_mx(
+                        out=bank[:, width * s : width * (s + 1)],
+                        lhsT=words[a][:, cols].bitcast(FP8X4),
+                        lhsT_scale=scales[a][:, cols],
+                        rhs=g_w[a][STARTS[c] // HALF][:, lo : lo + width].bitcast(FP8X4),
+                        rhs_scale=planes[a][:, STARTS[c] : STARTS[c] + width],
+                        start=(a == 0 and s == 0),
+                        stop=(closes and a == PASSES - 1 and s == len(tiles) - 1),
+                    )
 
-        def base_pass(a, c, u, bank):
-            chunk_pass(w1_w[a], w1_s[a], a, c, u, bank, a == 0, a == PASSES - 1)
-
-        cap = [[sb("cap%d_%d" % (h, u), [P, 2, HALF], F32) for u in range(2)] for h in range(2)]
-        low = [[sb("low%d_%d" % (c, u), [P, 2 * CHUNK], F32) for u in range(2)] for c in range(CHUNKS)]
-        hf = [sb("hf%d" % c, [P, 4 * CHUNK], F32) for c in range(CHUNKS)]
-        hb = [sb("hb%d" % c, [P, 4 * CHUNK], BF16) for c in range(CHUNKS)]
+        w3_planes = [w3_s[4 * a : P, :] for a in range(PASSES)]
+        cap = [sb("cap%d" % h, [P, 4, HALF], F32) for h in range(2)]
+        low = [sb("low%d" % c, [P, 4 * w], F32) for c, w in enumerate(WIDTHS)]
+        hf = [sb("hf%d" % c, [P, 4 * w], F32) for c, w in enumerate(WIDTHS)]
+        hb = [sb("hb%d" % c, [P, 4 * w], BF16) for c, w in enumerate(WIDTHS)]
+        y = [sb("y%d" % c, [P, 4 * w], F32) for c, w in enumerate(WIDTHS)]
         h_w = sb("h_w", [P, S], U32)
         h_s = sb("h_s", [P, S], U8)
-        y = [[sb("y%d_%d" % (c, u), [P, 2 * CHUNK], F32) for u in range(2)] for c in range(CHUNKS)]
         h_rows = out_1.rearrange("(p t) j -> p t j", t=4)
         y_rows = out_0.rearrange("(u p) j -> p u j", p=P)
 
-        def save_cap(h, t, bank):
-            nc.scalar.copy(cap[h][t // 2][:, t % 2, :], bank[:])
+        def floor_(c, group):
+            for u, b in enumerate(group):
+                table_passes(w3_w, w3_planes, c, u, banks[b], True)
 
-        def take_min(c, u, bank):
-            lo = CHUNK * (c % 2)
-            nc.vector.tensor_tensor(
-                low[c][u][:].rearrange("p (s j) -> p s j", s=2),
-                bank[:].rearrange("p (s j) -> p s j", s=2),
-                cap[c // 2][u][:, :, lo : lo + CHUNK],
-                ALU.min,
-            )
+        def base(c, group):
+            for u, b in enumerate(group):
+                table_passes(w1_w, w1_s, c, u, banks[b], True)
 
-        def take_max(c, u, bank):
-            nc.vector.tensor_tensor(hf[c][:, 512 * u : 512 * (u + 1)], bank[:], low[c][u][:], ALU.max)
+        def direct(c, group):
+            for u, b in enumerate(group):
+                table_passes(w5_w, w5_s, c, u, banks[b], False)
 
-        def store_h(c):
+        def take_min(c, group):
+            width, lo = WIDTHS[c], STARTS[c] % HALF
+            for u, b in enumerate(group):
+                tiles = tiles_of(c, u)
+                nc.vector.tensor_tensor(
+                    low[c][:, BANK * u : BANK * (u + 1)].rearrange("p (s j) -> p s j", j=width),
+                    banks[b][:].rearrange("p (s j) -> p s j", j=width),
+                    cap[STARTS[c] // HALF][:, tiles.start : tiles.stop, lo : lo + width],
+                    ALU.min,
+                )
+
+        def take_max(c, group):
+            for u, b in enumerate(group):
+                cols = slice(BANK * u, BANK * (u + 1))
+                nc.vector.tensor_tensor(hf[c][:, cols], banks[b][:], low[c][:, cols], ALU.max)
             nc.sync.dma_start(
-                out=h_rows[:, :, CHUNK * c : CHUNK * (c + 1)], in_=hf[c][:].rearrange("p (t j) -> p t j", t=4)
+                out=h_rows[:, :, STARTS[c] : STARTS[c] + WIDTHS[c]], in_=hf[c][:].rearrange("p (t j) -> p t j", t=4)
             )
 
         def round_h(c):
-            copy = nc.vector.tensor_copy if c == CHUNKS - 1 else nc.scalar.copy
+            copy = nc.vector.tensor_copy if c == len(WIDTHS) - 1 else nc.scalar.copy
             copy(
                 hb[c][:].rearrange("p (c i t) -> p c t i", i=4, t=4),
                 hf[c][:].rearrange("p (t c i) -> p c t i", t=4, i=4),
             )
 
         def quantize_h(c):
-            cols = slice(CHUNK * c, CHUNK * (c + 1))
+            cols = slice(STARTS[c], STARTS[c] + WIDTHS[c])
             nc.vector.quantize_mx(out=h_w[:, cols].bitcast(FP8X4), scales=h_s[:, cols], in_=hb[c][:])
 
-        def direct_passes(c, u, bank):
-            for a in range(PASSES):
-                chunk_pass(w5_w[a], w5_s[a], a, c, u, bank, a == 0, False)
-
-        def collar_passes(c, u, bank):
-            for s in range(2):
-                n = 2 * u + s
-                for k in range(2):
-                    cols = slice(CHUNK * c + P * k, CHUNK * c + P * (k + 1))
-                    nc.tensor.matmul_mx(
-                        out=bank[:, CHUNK * s + P * k : CHUNK * s + P * (k + 1)],
-                        lhsT=w4_w[:, 256 * n : 256 * (n + 1)].bitcast(FP4X4),
-                        lhsT_scale=w4_s[:, P * n : P * (n + 1)],
-                        rhs=h_w[:, cols].bitcast(FP8X4),
-                        rhs_scale=h_s[:, cols],
-                        start=False,
-                        stop=(s == 1 and k == 1),
-                    )
-
-        def finish(c, u, bank):
-            nc.scalar.activation(y[c][u][:], bank[:], ACT.Silu)
-            nc.sync.dma_start(
-                out=y_rows[:, 2 * u : 2 * u + 2, CHUNK * c : CHUNK * (c + 1)],
-                in_=y[c][u][:].rearrange("p (s j) -> p s j", s=2),
-            )
-
-        gather_scales()
-        load_late()
-        gather_words(0, 0)
-        deal_w3_scales()
-        deal_w3(0)
-        for c in range(2):
-            for u in range(2):
-                floor_pass(0, c, u, banks[4 + 2 * c + u])
-        deal_w3(1)
-        gather_words(1, 0)
-        for c in range(2):
-            for u in range(2):
-                floor_pass(1, c, u, banks[4 + 2 * c + u])
-        deal_w2(0)
-        deal_w2_scales()
-        deal_w2(1)
-        gather_words(0, 1)
-        gather_words(1, 1)
-        for h in range(2):
-            for t in range(4):
-                for a in range(PASSES):
-                    cap_pass(a, h, t, banks[t])
-                save_cap(h, t, banks[t])
-        for a in range(PASSES):
-            round_w1(a)
-            quantize_w1(a)
-
-        def base(c, pair):
-            for u in range(2):
-                for a in range(PASSES):
-                    base_pass(a, c, u, pair[u])
-
-        def floor_(c, pair):
-            for u in range(2):
-                for a in range(PASSES):
-                    floor_pass(a, c, u, pair[u])
-
-        def collar(c, base_pair, floor_pair):
-            for u in range(2):
-                take_min(c, u, base_pair[u])
-            for u in range(2):
-                take_max(c, u, floor_pair[u])
-            store_h(c)
-            round_h(c)
-
-        def direct(c, pair):
-            for u in range(2):
-                direct_passes(c, u, pair[u])
-
-        def second(c, pair):
-            for u in range(2):
-                collar_passes(c, u, pair[u])
-                finish(c, u, pair[u])
+        def second(c, group):
+            width = WIDTHS[c]
+            for u, b in enumerate(group):
+                tiles = tiles_of(c, u)
+                for s, n in enumerate(tiles):
+                    for k in range(width // P):
+                        cols = slice(STARTS[c] + P * k, STARTS[c] + P * (k + 1))
+                        nc.tensor.matmul_mx(
+                            out=banks[b][:, width * s + P * k : width * s + P * (k + 1)],
+                            lhsT=w4_w[:, 256 * n : 256 * (n + 1)].bitcast(FP4X4),
+                            lhsT_scale=w4_s[:, P * n : P * (n + 1)],
+                            rhs=h_w[:, cols].bitcast(FP8X4),
+                            rhs_scale=h_s[:, cols],
+                            start=False,
+                            stop=(s == len(tiles) - 1 and k == width // P - 1),
+                        )
+                cols = slice(BANK * u, BANK * (u + 1))
+                nc.scalar.activation(y[c][:, cols], banks[b][:], ACT.Silu)
+                nc.sync.dma_start(
+                    out=y_rows[:, tiles.start : tiles.stop, STARTS[c] : STARTS[c] + width],
+                    in_=y[c][:, cols].rearrange("p (s j) -> p s j", j=width),
+                )
 
         def store_words(h):
             cols = slice(HALF * h, HALF * (h + 1))
@@ -355,44 +287,95 @@ def tile_list_margin_collar_alert_kernel(
                 out=out_2[0].rearrange("p m t -> p (m t)").bitcast(I32)[:, cols], in_=h_w[:, cols].bitcast(I32)
             )
 
-        pa, pb, pc, pd = banks[0:2], banks[2:4], banks[4:6], banks[6:8]
-        for c in range(2):
-            for a in range(PASSES):
-                for u in range(2):
-                    base_pass(a, c, u, banks[2 * c + u])
+        nc.vector.tensor_copy(g_s[:], tab_s[:].indirect(offsets[:]))
+        nc.sync.dma_start(out=gs_low[0:100, :].bitcast(I32), in_=g_s[16:116, :].bitcast(I32))
+        nc.sync.dma_start(out=w1_late[:].rearrange("p (j c) -> p j c", j=4), in_=w1_first[:, :, 256:512])
+        gather_words(0, 0)
+        deal(ws[0][:], w2s_raw[:, 0:H])
+        deal(w2_w[0][:].bitcast(U16), w2_raw[:, 0 : 2 * H].bitcast(U16))
+        for t in range(4):
+            cap_pass(0, 0, t)
+        deal(w2_w[1][:].bitcast(U16), w2_raw[:, 2 * H : 4 * H].bitcast(U16))
+        deal(ws[1][:], w2s_raw[:, H : 2 * H])
+        gather_words(0, 1)
+        load_rows(w1_raw1, w1, 1)
+        load_rows(w5_raw[0], w5, 0)
+        for t in range(4):
+            cap_pass(0, 1, t)
+        round_w1_first(nc.scalar.copy, w1_early, 0)
+        gather_words(1, 0)
+        gather_words(1, 1)
+        for h in range(2):
+            for t in range(4):
+                cap_pass(1, h, t)
+                nc.scalar.copy(cap[h][:, t, :], banks[4 * h + t][:])
+        load_rows(w5_raw[1], w5, 1)
+        deal(w3_s[:], w3s_raw[:])
+        for a in range(PASSES):
+            deal(w3_w[a][:], w3_raw[:, H * a : H * (a + 1)])
+        nc.sync.dma_start(out=w4_w[:].bitcast(I32), in_=w4_words[0].bitcast(I32))
+        nc.gpsimd.memset(w4_s[:].bitcast(I32), 0)
+        for q in range(4):
+            nc.sync.dma_start(
+                out=w4_s[32 * q : 32 * q + 4, :].bitcast(I32),
+                in_=w4_scales[0, 4 * q : 4 * q + 4, :].bitcast(I32),
+            )
+        floor_(0, (0, 1))
+        round_w1_first(nc.vector.tensor_copy, w1_late, 1)
+        for u in range(2):
+            round_w1_second(u)
+            quantize_w(w1_w, w1_s, w1_b, 0, u)
+        for u in range(2):
+            quantize_w(w1_w, w1_s, w1_b, 1, u)
+        base(0, (2, 3))
+        floor_(1, (4, 5))
+        base(1, (6, 7))
+
         for u in range(2):
             round_w5(0, u)
-        collar(0, pa, pc)
+        round_w5(1, 0)
+        round_w5_pool(1, 1)
+        take_min(0, (2, 3))
+        take_max(0, (0, 1))
+        round_h(0)
+        base(2, (2, 3))
+        floor_(2, (0, 1))
         for u in range(2):
-            round_w5(1, u)
-        base(2, pa)
-        floor_(2, pc)
-        collar(1, pb, pd)
+            quantize_w(w5_w, w5_s, w5_b, 0, u)
+        take_min(1, (6, 7))
+        for u in range(2):
+            quantize_w(w5_w, w5_s, w5_b, 1, u)
         quantize_h(0)
-        for u in range(2):
-            for a in range(PASSES):
-                quantize_w5(a, u)
-        base(3, pb)
-        direct(0, pd)
-        second(0, pd)
-        collar(2, pa, pc)
+        take_max(1, (4, 5))
+        round_h(1)
+        base(3, (4,))
+        floor_(3, (5,))
+        direct(0, (6, 7))
+        second(0, (6, 7))
+        take_min(2, (2, 3))
         quantize_h(1)
         store_words(0)
-        floor_(3, pa)
-        direct(1, pc)
-        second(1, pc)
-        direct(2, pd)
-        for u in range(2):
-            take_min(3, u, pb[u])
-        quantize_h(2)
-        second(2, pd)
-        direct(3, pb)
-        for u in range(2):
-            take_max(3, u, pa[u])
-        store_h(3)
+        take_max(2, (0, 1))
+        round_h(2)
+        base(4, (2,))
+        floor_(4, (3,))
+        direct(1, (0, 1))
+        second(1, (0, 1))
+        take_min(3, (4,))
+        take_max(3, (5,))
         round_h(3)
+        direct(2, (6, 7))
+        take_min(4, (2,))
+        quantize_h(2)
+        second(2, (6, 7))
+        direct(3, (4,))
+        direct(4, (5,))
+        take_max(4, (3,))
+        round_h(4)
         quantize_h(3)
-        second(3, pb)
+        second(3, (4,))
+        quantize_h(4)
+        second(4, (5,))
         store_words(1)
         for q in range(4):
             nc.sync.dma_start(

@@ -74,6 +74,11 @@ def tile_list_margin_collar_alert_kernel(
         nc.vector.memset(zeros_c[:], 0)
         nc.vector.tensor_copy(gs_low[:].bitcast(I32), zeros_b[:])
         nc.vector.tensor_copy(w3s_raw[:].bitcast(I32), zeros_c[:])
+        idle_b = sb("idle_b", [P, 4 * HALF], BF16)
+        idle_w = sb("idle_w", [P, HALF], U32)
+        idle_s = sb("idle_s", [P, HALF], U8)
+        nc.gpsimd.memset(idle_b[:].bitcast(I32), 0)
+        nc.vector.quantize_mx(out=idle_w[:].bitcast(FP8X4), scales=idle_s[:], in_=idle_b[:])
         nc.gpsimd.memset(warm[:, 0:4], 0.0)
         nc.scalar.activation(warm[:, 4:8], warm[:, 0:4], ACT.Silu)
 
@@ -287,6 +292,16 @@ def tile_list_margin_collar_alert_kernel(
                 out=out_2[0].rearrange("p m t -> p (m t)").bitcast(I32)[:, cols], in_=h_w[:, cols].bitcast(I32)
             )
 
+        for i in range(6):
+            nc.tensor.matmul_mx(
+                out=banks[7][:],
+                lhsT=idle_w[:, 0:P].bitcast(FP8X4),
+                lhsT_scale=idle_s[:, 0:P],
+                rhs=idle_w[:].bitcast(FP8X4),
+                rhs_scale=tab_s[:, 0:HALF],
+                start=True,
+                stop=True,
+            )
         nc.vector.tensor_copy(g_s[:], tab_s[:].indirect(offsets[:]))
         nc.sync.dma_start(out=gs_low[0:100, :].bitcast(I32), in_=g_s[16:116, :].bitcast(I32))
         nc.sync.dma_start(out=w1_late[:].rearrange("p (j c) -> p j c", j=4), in_=w1_first[:, :, 256:512])

@@ -50,35 +50,27 @@ def tile_list_margin_collar_alert_kernel(
             return stage.tile(shape, dtype, name=name, offset=at, align_bytes=64)
 
         KB = 1024
-        tab_s = staged("tab_s", [P, T], U8, 0)
+        tab_s = staged("tab_s", [P, T], U8, 57 * KB + 512)
         zeros_a = staged("zeros_a", [P, 256], I32, 11 * KB)
         zeros_b = staged("zeros_b", [P, 256], I32, 26 * KB - 512)
-        zeros_c = staged("zeros_c", [P, 128], I32, 34 * KB)
         tab_w = [staged("tab_w0", [P, T], I32, 4 * KB), staged("tab_w1", [P, T], I32, 26 * KB)]
         w2_raw = staged("w2_raw", [P, PASSES * 2 * H], U8, 13 * KB)
-        w3_raw = staged("w3_raw", [P, PASSES * H], I32, 34 * KB)
+        w3_raw = staged("w3_raw", [P, PASSES * H], I32, 59 * KB)
         w2s_raw = staged("w2s_raw", [P, PASSES * H], U8, 38 * KB)
-        w3s_raw = staged("w3s_raw", [P, H], U8, 40 * KB)
-        g_w01 = staged("g_w01", [P, HALF], U32, 38 * KB)
+        w3s_raw = staged("w3s_raw", [P, H], U8, 58 * KB)
+        g_w01 = staged("g_w01", [P, HALF], U32, 36 * KB + 512)
         w1_early = staged("w1_early", [P, 2 * H], F32, 22 * KB)
-        w1_late = staged("w1_late", [P, 2 * H], F32, 0)
-        w1_raw1 = staged("w1_raw1", [P, 4 * H], F32, 14 * KB)
+        w1_late = staged("w1_late", [P, 2 * H], F32, 54 * KB)
+        w1_raw1 = staged("w1_raw1", [P, 4 * H], F32, 38 * KB + 512)
         w5_raw = [staged("w5_raw0", [P, 4 * N], F32, 4 * KB), staged("w5_raw1", [P, 4 * N], F32, 26 * KB)]
-        w4_w = staged("w4_w", [P, 2 * N], U8, 34 * KB)
+        w4_w = staged("w4_w", [P, 2 * N], U8, 39 * KB)
         w4_s = staged("w4_s", [P, N], U8, 40 * KB)
 
-        nc.gpsimd.memset(tab_s[:].bitcast(I32), 0)
         nc.vector.memset(zeros_a[:], 0)
+        nc.vector.memset(tab_s[:].bitcast(I32), 0)
         nc.vector.tensor_copy(w2s_raw[:].bitcast(I32), zeros_a[:])
         nc.vector.memset(zeros_b[:], 0)
-        nc.vector.memset(zeros_c[:], 0)
         nc.vector.tensor_copy(gs_low[:].bitcast(I32), zeros_b[:])
-        nc.vector.tensor_copy(w3s_raw[:].bitcast(I32), zeros_c[:])
-        idle_b = sb("idle_b", [P, 4 * HALF], BF16)
-        idle_w = sb("idle_w", [P, HALF], U32)
-        idle_s = sb("idle_s", [P, HALF], U8)
-        nc.gpsimd.memset(idle_b[:].bitcast(I32), 0)
-        nc.vector.quantize_mx(out=idle_w[:].bitcast(FP8X4), scales=idle_s[:], in_=idle_b[:])
         nc.gpsimd.memset(warm[:, 0:4], 0.0)
         nc.scalar.activation(warm[:, 4:8], warm[:, 0:4], ACT.Silu)
 
@@ -106,15 +98,6 @@ def tile_list_margin_collar_alert_kernel(
         w1_first = w1[0:512, :].rearrange("(p j) c -> p j c", j=4)
         nc.sync.dma_start(out=w1_early[:].rearrange("p (j c) -> p j c", j=4), in_=w1_first[:, :, 0:256])
         load_words(tab_w[1], tab_words[1])
-        nc.sync.dma_start(
-            out=w3_raw[:].rearrange("p (a c) -> p a c", a=PASSES),
-            in_=w3_words.rearrange("a p c i -> p a (c i)").bitcast(I32),
-        )
-        for q in range(4):
-            nc.sync.dma_start(
-                out=w3s_raw[32 * q : 32 * q + 8, :].bitcast(I32),
-                in_=w3_scales[:, 4 * q : 4 * q + 4, :].bitcast(I32),
-            )
 
         g_w = [
             [sb("g_w00", [P, HALF], U32), g_w01],
@@ -194,10 +177,10 @@ def tile_list_margin_collar_alert_kernel(
             per_bank = BANK // WIDTHS[c]
             return range(per_bank * u, per_bank * (u + 1))
 
-        def table_passes(words, scales, c, u, bank, closes):
+        def table_passes(words, scales, c, u, bank, closes, order=(0, 1)):
             width, lo = WIDTHS[c], STARTS[c] % HALF
             tiles = tiles_of(c, u)
-            for a in range(PASSES):
+            for a in order:
                 for s, t in enumerate(tiles):
                     cols = slice(P * t, P * (t + 1))
                     nc.tensor.matmul_mx(
@@ -206,8 +189,8 @@ def tile_list_margin_collar_alert_kernel(
                         lhsT_scale=scales[a][:, cols],
                         rhs=g_w[a][STARTS[c] // HALF][:, lo : lo + width].bitcast(FP8X4),
                         rhs_scale=planes[a][:, STARTS[c] : STARTS[c] + width],
-                        start=(a == 0 and s == 0),
-                        stop=(closes and a == PASSES - 1 and s == len(tiles) - 1),
+                        start=(a == order[0] and s == 0),
+                        stop=(closes and a == order[-1] and s == len(tiles) - 1),
                     )
 
         w3_planes = [w3_s[4 * a : P, :] for a in range(PASSES)]
@@ -227,7 +210,7 @@ def tile_list_margin_collar_alert_kernel(
 
         def base(c, group):
             for u, b in enumerate(group):
-                table_passes(w1_w, w1_s, c, u, banks[b], True)
+                table_passes(w1_w, w1_s, c, u, banks[b], True, (1, 0) if c else (0, 1))
 
         def direct(c, group):
             for u, b in enumerate(group):
@@ -292,19 +275,29 @@ def tile_list_margin_collar_alert_kernel(
                 out=out_2[0].rearrange("p m t -> p (m t)").bitcast(I32)[:, cols], in_=h_w[:, cols].bitcast(I32)
             )
 
-        for i in range(6):
+        nc.vector.tensor_copy(g_s[:], tab_s[:].indirect(offsets[:]))
+        nc.sync.dma_start(out=gs_low[0:100, :].bitcast(I32), in_=g_s[16:116, :].bitcast(I32))
+        nc.sync.dma_start(
+            out=w3_raw[:].rearrange("p (a c) -> p a c", a=PASSES),
+            in_=w3_words.rearrange("a p c i -> p a (c i)").bitcast(I32),
+        )
+        nc.vector.memset(w3s_raw[:].bitcast(I32), 0)
+        for q in range(4):
+            nc.sync.dma_start(
+                out=w3s_raw[32 * q : 32 * q + 8, :].bitcast(I32),
+                in_=w3_scales[:, 4 * q : 4 * q + 4, :].bitcast(I32),
+            )
+        nc.sync.dma_start(out=w1_late[:].rearrange("p (j c) -> p j c", j=4), in_=w1_first[:, :, 256:512])
+        for i in range(3):
             nc.tensor.matmul_mx(
                 out=banks[7][:],
-                lhsT=idle_w[:, 0:P].bitcast(FP8X4),
-                lhsT_scale=idle_s[:, 0:P],
-                rhs=idle_w[:].bitcast(FP8X4),
-                rhs_scale=tab_s[:, 0:HALF],
+                lhsT=w2_raw[:, 0 : 2 * P].bitcast(FP4X4),
+                lhsT_scale=g_s[:, 0:P],
+                rhs=tab_w[0][:, 0:HALF].bitcast(FP8X4),
+                rhs_scale=g_s[:, 0:HALF],
                 start=True,
                 stop=True,
             )
-        nc.vector.tensor_copy(g_s[:], tab_s[:].indirect(offsets[:]))
-        nc.sync.dma_start(out=gs_low[0:100, :].bitcast(I32), in_=g_s[16:116, :].bitcast(I32))
-        nc.sync.dma_start(out=w1_late[:].rearrange("p (j c) -> p j c", j=4), in_=w1_first[:, :, 256:512])
         gather_words(0, 0)
         deal(ws[0][:], w2s_raw[:, 0:H])
         deal(w2_w[0][:].bitcast(U16), w2_raw[:, 0 : 2 * H].bitcast(U16))
@@ -328,20 +321,21 @@ def tile_list_margin_collar_alert_kernel(
         deal(w3_s[:], w3s_raw[:])
         for a in range(PASSES):
             deal(w3_w[a][:], w3_raw[:, H * a : H * (a + 1)])
+        floor_(0, (0, 1))
+        round_w1_first(nc.vector.tensor_copy, w1_late, 1)
+        for u in range(2):
+            quantize_w(w1_w, w1_s, w1_b, 0, u)
+        for u in range(2):
+            round_w1_second(u)
+        for u in range(2):
+            quantize_w(w1_w, w1_s, w1_b, 1, u)
         nc.sync.dma_start(out=w4_w[:].bitcast(I32), in_=w4_words[0].bitcast(I32))
-        nc.gpsimd.memset(w4_s[:].bitcast(I32), 0)
+        nc.vector.memset(w4_s[:].bitcast(I32), 0)
         for q in range(4):
             nc.sync.dma_start(
                 out=w4_s[32 * q : 32 * q + 4, :].bitcast(I32),
                 in_=w4_scales[0, 4 * q : 4 * q + 4, :].bitcast(I32),
             )
-        floor_(0, (0, 1))
-        round_w1_first(nc.vector.tensor_copy, w1_late, 1)
-        for u in range(2):
-            round_w1_second(u)
-            quantize_w(w1_w, w1_s, w1_b, 0, u)
-        for u in range(2):
-            quantize_w(w1_w, w1_s, w1_b, 1, u)
         base(0, (2, 3))
         floor_(1, (4, 5))
         base(1, (6, 7))
@@ -355,34 +349,34 @@ def tile_list_margin_collar_alert_kernel(
         round_h(0)
         base(2, (2, 3))
         floor_(2, (0, 1))
-        for u in range(2):
-            quantize_w(w5_w, w5_s, w5_b, 0, u)
+        for a in range(PASSES):
+            quantize_w(w5_w, w5_s, w5_b, a, 0)
         take_min(1, (6, 7))
-        for u in range(2):
-            quantize_w(w5_w, w5_s, w5_b, 1, u)
+        for a in range(PASSES):
+            quantize_w(w5_w, w5_s, w5_b, a, 1)
         quantize_h(0)
+        direct(0, (6, 7))
+        second(0, (6, 7))
         take_max(1, (4, 5))
         round_h(1)
         base(3, (4,))
         floor_(3, (5,))
-        direct(0, (6, 7))
-        second(0, (6, 7))
+        direct(1, (6, 7))
         take_min(2, (2, 3))
         quantize_h(1)
+        second(1, (6, 7))
         store_words(0)
-        take_max(2, (0, 1))
-        round_h(2)
         base(4, (2,))
         floor_(4, (3,))
-        direct(1, (0, 1))
-        second(1, (0, 1))
+        take_max(2, (0, 1))
+        round_h(2)
+        direct(2, (0, 1))
         take_min(3, (4,))
         take_max(3, (5,))
         round_h(3)
-        direct(2, (6, 7))
         take_min(4, (2,))
         quantize_h(2)
-        second(2, (6, 7))
+        second(2, (0, 1))
         direct(3, (4,))
         direct(4, (5,))
         take_max(4, (3,))

@@ -20,7 +20,7 @@ P = 128
 PASSES = 2
 HALF = 512
 BANK = 512
-WIDTHS = (256, 256, 256, 128, 128)
+WIDTHS = (256, 256, 256, 256)
 STARTS = tuple(sum(WIDTHS[:c]) for c in range(len(WIDTHS)))
 
 
@@ -57,12 +57,15 @@ def tile_list_margin_collar_alert_kernel(
         w2_raw = staged("w2_raw", [P, PASSES * 2 * H], U8, 13 * KB)
         w3_raw = staged("w3_raw", [P, PASSES * H], I32, 59 * KB)
         w2s_raw = staged("w2s_raw", [P, PASSES * H], U8, 38 * KB)
-        w3s_raw = staged("w3s_raw", [P, H], U8, 58 * KB)
+        w3s_raw = sb("w3s_raw", [P, H], U8)
         g_w01 = staged("g_w01", [P, HALF], U32, 36 * KB + 512)
         w1_early = staged("w1_early", [P, 2 * H], F32, 22 * KB)
         w1_late = staged("w1_late", [P, 2 * H], F32, 54 * KB)
         w1_raw1 = staged("w1_raw1", [P, 4 * H], F32, 38 * KB + 512)
-        w5_raw = [staged("w5_raw0", [P, 4 * N], F32, 4 * KB), staged("w5_raw1", [P, 4 * N], F32, 26 * KB)]
+        w5_raw = [
+            [staged("w5_raw%d_%d" % (a, u), [P, 2 * N], F32, (4 + 4 * a + 22 * u) * KB) for u in range(2)]
+            for a in range(PASSES)
+        ]
         w4_w = staged("w4_w", [P, 2 * N], U8, 39 * KB)
         w4_s = staged("w4_s", [P, N], U8, 40 * KB)
 
@@ -71,6 +74,7 @@ def tile_list_margin_collar_alert_kernel(
         nc.vector.tensor_copy(w2s_raw[:].bitcast(I32), zeros_a[:])
         nc.vector.memset(zeros_b[:], 0)
         nc.vector.tensor_copy(gs_low[:].bitcast(I32), zeros_b[:])
+        nc.vector.tensor_copy(w3s_raw[:].bitcast(I32), zeros_b[:, 0:128])
         nc.gpsimd.memset(warm[:, 0:4], 0.0)
         nc.scalar.activation(warm[:, 4:8], warm[:, 0:4], ACT.Silu)
 
@@ -86,6 +90,13 @@ def tile_list_margin_collar_alert_kernel(
             out=w2_raw[:].bitcast(I32).rearrange("p (a c) -> p a c", a=PASSES),
             in_=w2_words.rearrange("a p c -> p a c").bitcast(I32),
         )
+        def load_w5(u):
+            for a in range(PASSES):
+                rows = w5[512 * a : 512 * (a + 1), :].rearrange("(p j) c -> p j c", j=4)
+                nc.sync.dma_start(
+                    out=w5_raw[a][u][:].rearrange("p (j c) -> p j c", j=4), in_=rows[:, :, 256 * u : 256 * (u + 1)]
+                )
+
         ts_rows = tab_scales.rearrange("a (q r) t -> r q a t", r=4)
         for r in range(4):
             nc.sync.dma_start(out=tab_s[r:P:16, :].bitcast(I32), in_=ts_rows[r].bitcast(I32))
@@ -98,6 +109,11 @@ def tile_list_margin_collar_alert_kernel(
         w1_first = w1[0:512, :].rearrange("(p j) c -> p j c", j=4)
         nc.sync.dma_start(out=w1_early[:].rearrange("p (j c) -> p j c", j=4), in_=w1_first[:, :, 0:256])
         load_words(tab_w[1], tab_words[1])
+        for q in range(4):
+            nc.sync.dma_start(
+                out=w3s_raw[32 * q : 32 * q + 8, :].bitcast(I32),
+                in_=w3_scales[:, 4 * q : 4 * q + 4, :].bitcast(I32),
+            )
 
         g_w = [
             [sb("g_w00", [P, HALF], U32), g_w01],
@@ -125,7 +141,10 @@ def tile_list_margin_collar_alert_kernel(
         w1_b.append([sb("w1_b1_%d" % u, [P, 2 * H], BF16) for u in range(2)])
         w1_w = [sb("w1_w%d" % a, [P, H], U32) for a in range(PASSES)]
         w1_s = [sb("w1_s%d" % a, [P, H], U8) for a in range(PASSES)]
-        w5_b = [[sb("w5_b%d_%d" % (a, u), [P, 2 * N], BF16) for u in range(2)] for a in range(PASSES)]
+        w5_b = [
+            [staged("w5_b%d_%d" % (a, u), [P, 2 * N], BF16, (64 + 2 * a + 4 * u) * KB) for u in range(2)]
+            for a in range(PASSES)
+        ]
         w5_w = [sb("w5_w%d" % a, [P, N], U32) for a in range(PASSES)]
         w5_s = [sb("w5_s%d" % a, [P, N], U8) for a in range(PASSES)]
 
@@ -144,15 +163,15 @@ def tile_list_margin_collar_alert_kernel(
         def round_w5(a, u):
             nc.scalar.copy(
                 w5_b[a][u][:].rearrange("p (c i j) -> p c j i", i=4, j=4),
-                w5_raw[a][:].rearrange("p (j c i) -> p c j i", j=4, i=4)[:, 64 * u : 64 * (u + 1), :, :],
+                w5_raw[a][u][:].rearrange("p (j c i) -> p c j i", j=4, i=4),
             )
 
         def round_w5_pool(a, u):
             for v in range(2):
-                lo = 256 * u + 128 * v
+                lo = 128 * v
                 nc.gpsimd.tensor_scalar(
                     w5_b[a][u][:, 512 * v : 512 * (v + 1)].rearrange("p (c j) -> p c j", j=4),
-                    w5_raw[a][:].rearrange("p (j c) -> p c j", j=4)[:, lo : lo + 128, :],
+                    w5_raw[a][u][:].rearrange("p (j c) -> p c j", j=4)[:, lo : lo + 128, :],
                     1.0, 0.0, ALU.mult, ALU.add,
                 )
 
@@ -195,9 +214,18 @@ def tile_list_margin_collar_alert_kernel(
 
         w3_planes = [w3_s[4 * a : P, :] for a in range(PASSES)]
         cap = [sb("cap%d" % h, [P, 4, HALF], F32) for h in range(2)]
-        low = [sb("low%d" % c, [P, 4 * w], F32) for c, w in enumerate(WIDTHS)]
-        hf = [sb("hf%d" % c, [P, 4 * w], F32) for c, w in enumerate(WIDTHS)]
-        hb = [sb("hb%d" % c, [P, 4 * w], BF16) for c, w in enumerate(WIDTHS)]
+
+        def chunk_tiles(name, dtype, places):
+            return [
+                staged("%s%d" % (name, c), [P, 4 * w], dtype, places[c] * KB)
+                if c in places
+                else sb("%s%d" % (name, c), [P, 4 * w], dtype)
+                for c, w in enumerate(WIDTHS)
+            ]
+
+        hb = chunk_tiles("hb", BF16, {0: 26})
+        low = chunk_tiles("low", F32, {1: 64, 2: 68})
+        hf = chunk_tiles("hf", F32, {})
         y = [sb("y%d" % c, [P, 4 * w], F32) for c, w in enumerate(WIDTHS)]
         h_w = sb("h_w", [P, S], U32)
         h_s = sb("h_s", [P, S], U8)
@@ -281,12 +309,6 @@ def tile_list_margin_collar_alert_kernel(
             out=w3_raw[:].rearrange("p (a c) -> p a c", a=PASSES),
             in_=w3_words.rearrange("a p c i -> p a (c i)").bitcast(I32),
         )
-        nc.vector.memset(w3s_raw[:].bitcast(I32), 0)
-        for q in range(4):
-            nc.sync.dma_start(
-                out=w3s_raw[32 * q : 32 * q + 8, :].bitcast(I32),
-                in_=w3_scales[:, 4 * q : 4 * q + 4, :].bitcast(I32),
-            )
         nc.sync.dma_start(out=w1_late[:].rearrange("p (j c) -> p j c", j=4), in_=w1_first[:, :, 256:512])
         for i in range(3):
             nc.tensor.matmul_mx(
@@ -307,7 +329,7 @@ def tile_list_margin_collar_alert_kernel(
         deal(ws[1][:], w2s_raw[:, H : 2 * H])
         gather_words(0, 1)
         load_rows(w1_raw1, w1, 1)
-        load_rows(w5_raw[0], w5, 0)
+        load_w5(0)
         for t in range(4):
             cap_pass(0, 1, t)
         round_w1_first(nc.scalar.copy, w1_early, 0)
@@ -317,14 +339,13 @@ def tile_list_margin_collar_alert_kernel(
             for t in range(4):
                 cap_pass(1, h, t)
                 nc.scalar.copy(cap[h][:, t, :], banks[4 * h + t][:])
-        load_rows(w5_raw[1], w5, 1)
+        load_w5(1)
         deal(w3_s[:], w3s_raw[:])
         for a in range(PASSES):
             deal(w3_w[a][:], w3_raw[:, H * a : H * (a + 1)])
         floor_(0, (0, 1))
         round_w1_first(nc.vector.tensor_copy, w1_late, 1)
-        for u in range(2):
-            quantize_w(w1_w, w1_s, w1_b, 0, u)
+        nc.vector.quantize_mx(out=w1_w[0][:].bitcast(FP8X4), scales=w1_s[0][:], in_=w1_b0[:])
         for u in range(2):
             round_w1_second(u)
         for u in range(2):
@@ -340,9 +361,9 @@ def tile_list_margin_collar_alert_kernel(
         floor_(1, (4, 5))
         base(1, (6, 7))
 
-        for u in range(2):
-            round_w5(0, u)
-        round_w5(1, 0)
+        for a in range(PASSES):
+            round_w5(a, 0)
+        round_w5(0, 1)
         round_w5_pool(1, 1)
         take_min(0, (2, 3))
         take_max(0, (0, 1))
@@ -352,39 +373,31 @@ def tile_list_margin_collar_alert_kernel(
         for a in range(PASSES):
             quantize_w(w5_w, w5_s, w5_b, a, 0)
         take_min(1, (6, 7))
-        for a in range(PASSES):
-            quantize_w(w5_w, w5_s, w5_b, a, 1)
-        quantize_h(0)
-        direct(0, (6, 7))
-        second(0, (6, 7))
         take_max(1, (4, 5))
         round_h(1)
-        base(3, (4,))
-        floor_(3, (5,))
-        direct(1, (6, 7))
+        quantize_h(0)
+        for a in range(PASSES):
+            quantize_w(w5_w, w5_s, w5_b, a, 1)
+        direct(0, (6, 7))
+        second(0, (6, 7))
+        base(3, (4, 5))
         take_min(2, (2, 3))
         quantize_h(1)
-        second(1, (6, 7))
         store_words(0)
-        base(4, (2,))
-        floor_(4, (3,))
+        floor_(3, (2, 3))
+        direct(1, (6, 7))
+        second(1, (6, 7))
         take_max(2, (0, 1))
         round_h(2)
         direct(2, (0, 1))
-        take_min(3, (4,))
-        take_max(3, (5,))
-        round_h(3)
-        take_min(4, (2,))
+        take_min(3, (4, 5))
+        direct(3, (4, 5))
         quantize_h(2)
         second(2, (0, 1))
-        direct(3, (4,))
-        direct(4, (5,))
-        take_max(4, (3,))
-        round_h(4)
+        take_max(3, (2, 3))
+        round_h(3)
         quantize_h(3)
-        second(3, (4,))
-        quantize_h(4)
-        second(4, (5,))
+        second(3, (4, 5))
         store_words(1)
         for q in range(4):
             nc.sync.dma_start(

@@ -52,15 +52,14 @@ def tile_list_margin_collar_alert_kernel(
         KB = 1024
         tab_s = staged("tab_s", [P, T], U8, 57 * KB + 512)
         zeros_a = staged("zeros_a", [P, 256], I32, 11 * KB)
-        zeros_b = staged("zeros_b", [P, 256], I32, 26 * KB - 512)
+        zeros_b = staged("zeros_b", [P, 256], I32, 34 * KB - 512)
         tab_w = [staged("tab_w0", [P, T], I32, 4 * KB), staged("tab_w1", [P, T], I32, 26 * KB)]
         w2_raw = staged("w2_raw", [P, PASSES * 2 * H], U8, 13 * KB)
-        w3_raw = staged("w3_raw", [P, PASSES * H], I32, 59 * KB)
-        w2s_raw = staged("w2s_raw", [P, PASSES * H], U8, 38 * KB)
+        w3_raw = staged("w3_raw", [P, PASSES * H], I32, 34 * KB)
+        w2s_raw = staged("w2s_raw", [P, PASSES * H], U8, 46 * KB)
         w3s_raw = sb("w3s_raw", [P, H], U8)
-        g_w01 = staged("g_w01", [P, HALF], U32, 36 * KB + 512)
-        w1_early = staged("w1_early", [P, 2 * H], F32, 22 * KB)
-        w1_late = staged("w1_late", [P, 2 * H], F32, 54 * KB)
+        g_w01 = staged("g_w01", [P, HALF], U32, 46 * KB + 512)
+        w1_raw0 = staged("w1_raw0", [P, 4 * H], F32, 50 * KB)
         w1_raw1 = staged("w1_raw1", [P, 4 * H], F32, 38 * KB + 512)
         w5_raw = [
             [staged("w5_raw%d_%d" % (a, u), [P, 2 * N], F32, (4 + 4 * a + 22 * u) * KB) for u in range(2)]
@@ -69,8 +68,8 @@ def tile_list_margin_collar_alert_kernel(
         w4_w = staged("w4_w", [P, 2 * N], U8, 39 * KB)
         w4_s = staged("w4_s", [P, N], U8, 40 * KB)
 
-        nc.vector.memset(zeros_a[:], 0)
         nc.vector.memset(tab_s[:].bitcast(I32), 0)
+        nc.vector.memset(zeros_a[:], 0)
         nc.vector.tensor_copy(w2s_raw[:].bitcast(I32), zeros_a[:])
         nc.vector.memset(zeros_b[:], 0)
         nc.vector.tensor_copy(gs_low[:].bitcast(I32), zeros_b[:])
@@ -106,9 +105,11 @@ def tile_list_margin_collar_alert_kernel(
                 out=w2s_raw[32 * q : 32 * q + 4, :].bitcast(I32).rearrange("r (a c) -> r a c", a=PASSES),
                 in_=w2_scales[:, 4 * q : 4 * q + 4, :].rearrange("a r c -> r a c").bitcast(I32),
             )
-        w1_first = w1[0:512, :].rearrange("(p j) c -> p j c", j=4)
-        nc.sync.dma_start(out=w1_early[:].rearrange("p (j c) -> p j c", j=4), in_=w1_first[:, :, 0:256])
         load_words(tab_w[1], tab_words[1])
+        nc.sync.dma_start(
+            out=w3_raw[:].rearrange("p (a c) -> p a c", a=PASSES),
+            in_=w3_words.rearrange("a p c i -> p a (c i)").bitcast(I32),
+        )
         for q in range(4):
             nc.sync.dma_start(
                 out=w3s_raw[32 * q : 32 * q + 8, :].bitcast(I32),
@@ -148,10 +149,10 @@ def tile_list_margin_collar_alert_kernel(
         w5_w = [sb("w5_w%d" % a, [P, N], U32) for a in range(PASSES)]
         w5_s = [sb("w5_s%d" % a, [P, N], U8) for a in range(PASSES)]
 
-        def round_w1_first(copy, raw, v):
-            copy(
-                w1_b0[:].rearrange("p (t m j) -> p m j t", t=4, j=4)[:, 64 * v : 64 * (v + 1), :, :],
-                raw[:].rearrange("p (j m t) -> p m j t", j=4, t=4),
+        def round_w1_first():
+            nc.vector.tensor_copy(
+                w1_b0[:].rearrange("p (t m j) -> p m j t", t=4, j=4),
+                w1_raw0[:].rearrange("p (j m t) -> p m j t", j=4, t=4),
             )
 
         def round_w1_second(u):
@@ -305,11 +306,7 @@ def tile_list_margin_collar_alert_kernel(
 
         nc.vector.tensor_copy(g_s[:], tab_s[:].indirect(offsets[:]))
         nc.sync.dma_start(out=gs_low[0:100, :].bitcast(I32), in_=g_s[16:116, :].bitcast(I32))
-        nc.sync.dma_start(
-            out=w3_raw[:].rearrange("p (a c) -> p a c", a=PASSES),
-            in_=w3_words.rearrange("a p c i -> p a (c i)").bitcast(I32),
-        )
-        nc.sync.dma_start(out=w1_late[:].rearrange("p (j c) -> p j c", j=4), in_=w1_first[:, :, 256:512])
+        load_rows(w1_raw0, w1, 0)
         for i in range(3):
             nc.tensor.matmul_mx(
                 out=banks[7][:],
@@ -332,7 +329,6 @@ def tile_list_margin_collar_alert_kernel(
         load_w5(0)
         for t in range(4):
             cap_pass(0, 1, t)
-        round_w1_first(nc.scalar.copy, w1_early, 0)
         gather_words(1, 0)
         gather_words(1, 1)
         for h in range(2):
@@ -344,7 +340,7 @@ def tile_list_margin_collar_alert_kernel(
         for a in range(PASSES):
             deal(w3_w[a][:], w3_raw[:, H * a : H * (a + 1)])
         floor_(0, (0, 1))
-        round_w1_first(nc.vector.tensor_copy, w1_late, 1)
+        round_w1_first()
         nc.vector.quantize_mx(out=w1_w[0][:].bitcast(FP8X4), scales=w1_s[0][:], in_=w1_b0[:])
         for u in range(2):
             round_w1_second(u)

@@ -20,7 +20,7 @@ P = 128
 PASSES = 2
 HALF = 512
 BANK = 512
-WIDTHS = (256, 256, 256, 256)
+WIDTHS = (512, 256, 256)
 STARTS = tuple(sum(WIDTHS[:c]) for c in range(len(WIDTHS)))
 
 
@@ -50,7 +50,7 @@ def tile_list_margin_collar_alert_kernel(
             return stage.tile(shape, dtype, name=name, offset=at, align_bytes=64)
 
         KB = 1024
-        tab_s = staged("tab_s", [P, T], U8, 57 * KB + 512)
+        tab_s = staged("tab_s", [P, T], U8, 97 * KB + 512)
         zeros_a = staged("zeros_a", [P, 256], I32, 11 * KB)
         zeros_b = staged("zeros_b", [P, 256], I32, 34 * KB - 512)
         tab_w = [staged("tab_w0", [P, T], I32, 4 * KB), staged("tab_w1", [P, T], I32, 26 * KB)]
@@ -59,14 +59,16 @@ def tile_list_margin_collar_alert_kernel(
         w2s_raw = staged("w2s_raw", [P, PASSES * H], U8, 46 * KB)
         w3s_raw = sb("w3s_raw", [P, H], U8)
         g_w01 = staged("g_w01", [P, HALF], U32, 46 * KB + 512)
-        w1_raw0 = staged("w1_raw0", [P, 4 * H], F32, 50 * KB)
-        w1_raw1 = staged("w1_raw1", [P, 4 * H], F32, 38 * KB + 512)
+        w1_raw0 = staged("w1_raw0", [P, 4 * H], F32, 90 * KB)
+        w1_raw1 = [
+            staged("w1_raw1_0", [P, 2 * H], F32, 99 * KB),
+            staged("w1_raw1_1", [P, 2 * H], F32, 42 * KB + 512),
+        ]
         w5_raw = [
             [staged("w5_raw%d_%d" % (a, u), [P, 2 * N], F32, (4 + 4 * a + 22 * u) * KB) for u in range(2)]
             for a in range(PASSES)
         ]
-        w4_w = staged("w4_w", [P, 2 * N], U8, 39 * KB)
-        w4_s = staged("w4_s", [P, N], U8, 40 * KB)
+        w4_w = staged("w4_w", [P, 2 * N], U8, 43 * KB)
 
         nc.vector.memset(tab_s[:].bitcast(I32), 0)
         nc.vector.memset(zeros_a[:], 0)
@@ -89,6 +91,12 @@ def tile_list_margin_collar_alert_kernel(
             out=w2_raw[:].bitcast(I32).rearrange("p (a c) -> p a c", a=PASSES),
             in_=w2_words.rearrange("a p c -> p a c").bitcast(I32),
         )
+        def load_w1_second(v):
+            rows = w1[512:1024, :].rearrange("(p j) c -> p j c", j=4)
+            nc.sync.dma_start(
+                out=w1_raw1[v][:].rearrange("p (j c) -> p j c", j=4), in_=rows[:, :, 256 * v : 256 * (v + 1)]
+            )
+
         def load_w5(u):
             for a in range(PASSES):
                 rows = w5[512 * a : 512 * (a + 1), :].rearrange("(p j) c -> p j c", j=4)
@@ -117,7 +125,7 @@ def tile_list_margin_collar_alert_kernel(
             )
 
         g_w = [
-            [sb("g_w00", [P, HALF], U32), g_w01],
+            [staged("g_w00", [P, HALF], U32, 72 * KB), g_w01],
             [sb("g_w10", [P, HALF], U32), sb("g_w11", [P, HALF], U32)],
         ]
         planes = [g_s, gs_low]
@@ -129,25 +137,24 @@ def tile_list_margin_collar_alert_kernel(
 
         w3_s = sb("w3_s", [P, H], U8)
         ws = [sb("ws%d" % a, [P, H], U8) for a in range(PASSES)]
-        w3_w = [sb("w3_w%d" % a, [P, H], I32) for a in range(PASSES)]
-        w2_w = [sb("w2_w%d" % a, [P, 2 * H], U8) for a in range(PASSES)]
+        w3_w = [sb("w3_w0", [P, H], I32), sb("w3_w1", [P, H], I32)]
+        w2_w = [sb("w2_w0", [P, 2 * H], U8), staged("w2_w1", [P, 2 * H], U8, 76 * KB)]
+        w4_s = ws[1]
 
         def deal(dst, src):
             nc.vector.tensor_copy(
                 dst.rearrange("p (a t m) -> p a m t", t=4, m=P), src.rearrange("p (a m t) -> p a m t", t=4, m=P)
             )
 
+        w1_b1 = sb("w1_b1", [P, 4 * H], BF16)
         w1_b0 = sb("w1_b0", [P, 4 * H], BF16)
-        w1_b = [[w1_b0[:, 0 : 2 * H], w1_b0[:, 2 * H : 4 * H]]]
-        w1_b.append([sb("w1_b1_%d" % u, [P, 2 * H], BF16) for u in range(2)])
-        w1_w = [sb("w1_w%d" % a, [P, H], U32) for a in range(PASSES)]
+        w1_b = [None, [w1_b1[:, 0 : 2 * H], w1_b1[:, 2 * H : 4 * H]]]
+        w1_w = [sb("w1_w0", [P, H], U32), sb("w1_w1", [P, H], U32)]
         w1_s = [sb("w1_s%d" % a, [P, H], U8) for a in range(PASSES)]
-        w5_b = [
-            [staged("w5_b%d_%d" % (a, u), [P, 2 * N], BF16, (64 + 2 * a + 4 * u) * KB) for u in range(2)]
-            for a in range(PASSES)
-        ]
-        w5_w = [sb("w5_w%d" % a, [P, N], U32) for a in range(PASSES)]
-        w5_s = [sb("w5_s%d" % a, [P, N], U8) for a in range(PASSES)]
+        w5_both = [staged("w5_b0", [P, 4 * N], BF16, 64 * KB), staged("w5_b1", [P, 4 * N], BF16, 80 * KB)]
+        w5_b = [[w5_both[u][:, 2 * N * a : 2 * N * (a + 1)] for u in range(2)] for a in range(PASSES)]
+        w5_w = [sb("w5_w0", [P, N], U32), staged("w5_w1", [P, N], U32, 107 * KB)]
+        w5_s = [sb("w5_s%d" % u, [P, N], U8) for u in range(2)]
 
         def round_w1_first():
             nc.vector.tensor_copy(
@@ -155,10 +162,10 @@ def tile_list_margin_collar_alert_kernel(
                 w1_raw0[:].rearrange("p (j m t) -> p m j t", j=4, t=4),
             )
 
-        def round_w1_second(u):
+        def round_w1_second(v):
             nc.vector.tensor_copy(
-                w1_b[1][u][:].rearrange("p (t m j) -> p m j t", t=2, j=4),
-                w1_raw1[:].rearrange("p (j m t) -> p m j t", j=4, t=4)[:, :, :, 2 * u : 2 * u + 2],
+                w1_b1[:].rearrange("p (t m j) -> p m j t", t=4, j=4)[:, 64 * v : 64 * (v + 1), :, :],
+                w1_raw1[v][:].rearrange("p (j m t) -> p m j t", j=4, t=4),
             )
 
         def round_w5(a, u):
@@ -167,20 +174,14 @@ def tile_list_margin_collar_alert_kernel(
                 w5_raw[a][u][:].rearrange("p (j c i) -> p c j i", j=4, i=4),
             )
 
-        def round_w5_pool(a, u):
-            for v in range(2):
-                lo = 128 * v
-                nc.gpsimd.tensor_scalar(
-                    w5_b[a][u][:, 512 * v : 512 * (v + 1)].rearrange("p (c j) -> p c j", j=4),
-                    w5_raw[a][u][:].rearrange("p (j c) -> p c j", j=4)[:, lo : lo + 128, :],
-                    1.0, 0.0, ALU.mult, ALU.add,
-                )
-
         def quantize_w(words, scales, rounded, a, u):
             cols = slice(256 * u, 256 * (u + 1))
             nc.vector.quantize_mx(
                 out=words[a][:, cols].bitcast(FP8X4), scales=scales[a][:, cols], in_=rounded[a][u][:]
             )
+
+        def quantize_w5(u):
+            nc.vector.quantize_mx(out=w5_w[u][:].bitcast(FP8X4), scales=w5_s[u][:], in_=w5_both[u][:])
 
         def cap_pass(a, h, t):
             nc.tensor.matmul_mx(
@@ -197,10 +198,12 @@ def tile_list_margin_collar_alert_kernel(
             per_bank = BANK // WIDTHS[c]
             return range(per_bank * u, per_bank * (u + 1))
 
-        def table_passes(words, scales, c, u, bank, closes, order=(0, 1)):
+        def table_passes(words, scales, c, u, bank, closes, order=(0, 1), only=(0, 1)):
             width, lo = WIDTHS[c], STARTS[c] % HALF
             tiles = tiles_of(c, u)
             for a in order:
+                if a not in only:
+                    continue
                 for s, t in enumerate(tiles):
                     cols = slice(P * t, P * (t + 1))
                     nc.tensor.matmul_mx(
@@ -224,8 +227,12 @@ def tile_list_margin_collar_alert_kernel(
                 for c, w in enumerate(WIDTHS)
             ]
 
-        hb = chunk_tiles("hb", BF16, {0: 26})
-        low = chunk_tiles("low", F32, {1: 64, 2: 68})
+        hb = chunk_tiles("hb", BF16, {0: 104})
+        low = [
+            [sb("low0_%d" % u, [P, BANK], F32) for u in range(4)],
+            [sb("low1_%d" % u, [P, BANK], F32) for u in range(2)],
+            [staged("low2_%d" % u, [P, BANK], F32, (103 + 2 * u) * KB) for u in range(2)],
+        ]
         hf = chunk_tiles("hf", F32, {})
         y = [sb("y%d" % c, [P, 4 * w], F32) for c, w in enumerate(WIDTHS)]
         h_w = sb("h_w", [P, S], U32)
@@ -233,36 +240,46 @@ def tile_list_margin_collar_alert_kernel(
         h_rows = out_1.rearrange("(p t) j -> p t j", t=4)
         y_rows = out_0.rearrange("(u p) j -> p u j", p=P)
 
-        def floor_(c, group):
-            for u, b in enumerate(group):
-                table_passes(w3_w, w3_planes, c, u, banks[b], True)
+        def floor_(c, u, b):
+            table_passes(w3_w, w3_planes, c, u, banks[b], True)
 
-        def base(c, group):
-            for u, b in enumerate(group):
-                table_passes(w1_w, w1_s, c, u, banks[b], True, (1, 0) if c else (0, 1))
+        def base(c, u, b):
+            table_passes(w1_w, w1_s, c, u, banks[b], True, (1, 0))
 
-        def direct(c, group):
-            for u, b in enumerate(group):
-                table_passes(w5_w, w5_s, c, u, banks[b], False)
-
-        def take_min(c, group):
+        def direct(c, u, b):
             width, lo = WIDTHS[c], STARTS[c] % HALF
-            for u, b in enumerate(group):
-                tiles = tiles_of(c, u)
-                nc.vector.tensor_tensor(
-                    low[c][:, BANK * u : BANK * (u + 1)].rearrange("p (s j) -> p s j", j=width),
-                    banks[b][:].rearrange("p (s j) -> p s j", j=width),
-                    cap[STARTS[c] // HALF][:, tiles.start : tiles.stop, lo : lo + width],
-                    ALU.min,
-                )
+            for a in range(PASSES):
+                for s, n in enumerate(tiles_of(c, u)):
+                    cols = slice(256 * a + P * (n % 2), 256 * a + P * (n % 2 + 1))
+                    nc.tensor.matmul_mx(
+                        out=banks[b][:, width * s : width * (s + 1)],
+                        lhsT=w5_w[n // 2][:, cols].bitcast(FP8X4),
+                        lhsT_scale=w5_s[n // 2][:, cols],
+                        rhs=g_w[a][STARTS[c] // HALF][:, lo : lo + width].bitcast(FP8X4),
+                        rhs_scale=planes[a][:, STARTS[c] : STARTS[c] + width],
+                        start=(a == 0 and s == 0),
+                        stop=False,
+                    )
 
-        def take_max(c, group):
-            for u, b in enumerate(group):
-                cols = slice(BANK * u, BANK * (u + 1))
-                nc.vector.tensor_tensor(hf[c][:, cols], banks[b][:], low[c][:, cols], ALU.max)
-            nc.sync.dma_start(
-                out=h_rows[:, :, STARTS[c] : STARTS[c] + WIDTHS[c]], in_=hf[c][:].rearrange("p (t j) -> p t j", t=4)
+        def take_min(c, u, b):
+            width, lo = WIDTHS[c], STARTS[c] % HALF
+            tiles = tiles_of(c, u)
+            nc.vector.tensor_tensor(
+                low[c][u][:].rearrange("p (s j) -> p s j", j=width),
+                banks[b][:].rearrange("p (s j) -> p s j", j=width),
+                cap[STARTS[c] // HALF][:, tiles.start : tiles.stop, lo : lo + width],
+                ALU.min,
             )
+
+        def take_max(c, u, b):
+            cols = slice(BANK * u, BANK * (u + 1))
+            nc.vector.tensor_tensor(hf[c][:, cols], banks[b][:], low[c][u][:], ALU.max)
+            if u % 2:
+                rows = slice(u - 1, u + 1) if c == 0 else slice(0, 4)
+                nc.sync.dma_start(
+                    out=h_rows[:, rows, STARTS[c] : STARTS[c] + WIDTHS[c]],
+                    in_=hf[c][:].rearrange("p (t j) -> p t j", t=4)[:, rows, :],
+                )
 
         def round_h(c):
             copy = nc.vector.tensor_copy if c == len(WIDTHS) - 1 else nc.scalar.copy
@@ -274,39 +291,39 @@ def tile_list_margin_collar_alert_kernel(
         def quantize_h(c):
             cols = slice(STARTS[c], STARTS[c] + WIDTHS[c])
             nc.vector.quantize_mx(out=h_w[:, cols].bitcast(FP8X4), scales=h_s[:, cols], in_=hb[c][:])
-
-        def second(c, group):
-            width = WIDTHS[c]
-            for u, b in enumerate(group):
-                tiles = tiles_of(c, u)
-                for s, n in enumerate(tiles):
-                    for k in range(width // P):
-                        cols = slice(STARTS[c] + P * k, STARTS[c] + P * (k + 1))
-                        nc.tensor.matmul_mx(
-                            out=banks[b][:, width * s + P * k : width * s + P * (k + 1)],
-                            lhsT=w4_w[:, 256 * n : 256 * (n + 1)].bitcast(FP4X4),
-                            lhsT_scale=w4_s[:, P * n : P * (n + 1)],
-                            rhs=h_w[:, cols].bitcast(FP8X4),
-                            rhs_scale=h_s[:, cols],
-                            start=False,
-                            stop=(s == len(tiles) - 1 and k == width // P - 1),
-                        )
-                cols = slice(BANK * u, BANK * (u + 1))
-                nc.scalar.activation(y[c][:, cols], banks[b][:], ACT.Silu)
+            if c != 1:
+                half = slice(HALF * (c // 2), HALF * (c // 2 + 1))
                 nc.sync.dma_start(
-                    out=y_rows[:, tiles.start : tiles.stop, STARTS[c] : STARTS[c] + width],
-                    in_=y[c][:, cols].rearrange("p (s j) -> p s j", j=width),
+                    out=out_2[0].rearrange("p m t -> p (m t)").bitcast(I32)[:, half], in_=h_w[:, half].bitcast(I32)
                 )
 
-        def store_words(h):
-            cols = slice(HALF * h, HALF * (h + 1))
+        def finish(c, u, b):
+            width = WIDTHS[c]
+            step = BANK if width == BANK else P
+            tiles = tiles_of(c, u)
+            for s, n in enumerate(tiles):
+                for k in range(width // step):
+                    cols = slice(STARTS[c] + step * k, STARTS[c] + step * (k + 1))
+                    nc.tensor.matmul_mx(
+                        out=banks[b][:, width * s + step * k : width * s + step * (k + 1)],
+                        lhsT=w4_w[:, 256 * n : 256 * (n + 1)].bitcast(FP4X4),
+                        lhsT_scale=w4_s[:, P * n : P * (n + 1)],
+                        rhs=h_w[:, cols].bitcast(FP8X4),
+                        rhs_scale=h_s[:, cols],
+                        start=False,
+                        stop=(s == len(tiles) - 1 and k == width // step - 1),
+                    )
+            cols = slice(BANK * u, BANK * (u + 1))
+            nc.scalar.activation(y[c][:, cols], banks[b][:], ACT.Silu)
             nc.sync.dma_start(
-                out=out_2[0].rearrange("p m t -> p (m t)").bitcast(I32)[:, cols], in_=h_w[:, cols].bitcast(I32)
+                out=y_rows[:, tiles.start : tiles.stop, STARTS[c] : STARTS[c] + width],
+                in_=y[c][:, cols].rearrange("p (s j) -> p s j", j=width),
             )
 
         nc.vector.tensor_copy(g_s[:], tab_s[:].indirect(offsets[:]))
         nc.sync.dma_start(out=gs_low[0:100, :].bitcast(I32), in_=g_s[16:116, :].bitcast(I32))
         load_rows(w1_raw0, w1, 0)
+        load_w1_second(0)
         for i in range(3):
             nc.tensor.matmul_mx(
                 out=banks[7][:],
@@ -325,7 +342,7 @@ def tile_list_margin_collar_alert_kernel(
         deal(w2_w[1][:].bitcast(U16), w2_raw[:, 2 * H : 4 * H].bitcast(U16))
         deal(ws[1][:], w2s_raw[:, H : 2 * H])
         gather_words(0, 1)
-        load_rows(w1_raw1, w1, 1)
+        load_w1_second(1)
         load_w5(0)
         for t in range(4):
             cap_pass(0, 1, t)
@@ -334,67 +351,81 @@ def tile_list_margin_collar_alert_kernel(
         for h in range(2):
             for t in range(4):
                 cap_pass(1, h, t)
-                nc.scalar.copy(cap[h][:, t, :], banks[4 * h + t][:])
+        for b in range(8):
+            nc.scalar.copy(cap[b // 4][:, b % 4, :], banks[b][:])
         load_w5(1)
-        deal(w3_s[:], w3s_raw[:])
-        for a in range(PASSES):
-            deal(w3_w[a][:], w3_raw[:, H * a : H * (a + 1)])
-        floor_(0, (0, 1))
-        round_w1_first()
-        nc.vector.quantize_mx(out=w1_w[0][:].bitcast(FP8X4), scales=w1_s[0][:], in_=w1_b0[:])
-        for u in range(2):
-            round_w1_second(u)
-        for u in range(2):
-            quantize_w(w1_w, w1_s, w1_b, 1, u)
-        nc.sync.dma_start(out=w4_w[:].bitcast(I32), in_=w4_words[0].bitcast(I32))
-        nc.vector.memset(w4_s[:].bitcast(I32), 0)
         for q in range(4):
             nc.sync.dma_start(
                 out=w4_s[32 * q : 32 * q + 4, :].bitcast(I32),
                 in_=w4_scales[0, 4 * q : 4 * q + 4, :].bitcast(I32),
             )
-        base(0, (2, 3))
-        floor_(1, (4, 5))
-        base(1, (6, 7))
+        deal(w3_s[:], w3s_raw[:])
+        for a in range(PASSES):
+            deal(w3_w[a][:], w3_raw[:, H * a : H * (a + 1)])
+        for t in range(4):
+            floor_(0, t, t)
+        round_w1_first()
+        nc.vector.quantize_mx(out=w1_w[0][:].bitcast(FP8X4), scales=w1_s[0][:], in_=w1_b0[:])
+        for v in range(2):
+            round_w1_second(v)
+        for u in range(2):
+            quantize_w(w1_w, w1_s, w1_b, 1, u)
+        nc.sync.dma_start(out=w4_w[:].bitcast(I32), in_=w4_words[0].bitcast(I32))
+        for a in range(PASSES):
+            for t in range(4):
+                table_passes(w1_w, w1_s, 0, t, banks[4 + t], True, (0, 1), (a,))
 
-        for a in range(PASSES):
-            round_w5(a, 0)
-        round_w5(0, 1)
-        round_w5_pool(1, 1)
-        take_min(0, (2, 3))
-        take_max(0, (0, 1))
+        for u in range(2):
+            for a in range(PASSES):
+                round_w5(a, u)
+        take_min(0, 0, 4)
+        base(1, 0, 4)
+        take_min(0, 1, 5)
+        base(1, 1, 5)
+        take_max(0, 0, 0)
+        floor_(1, 0, 0)
+        take_min(0, 2, 6)
+        floor_(1, 1, 6)
+        take_max(0, 1, 1)
+        base(2, 0, 1)
+        take_min(0, 3, 7)
+        base(2, 1, 7)
+        take_max(0, 2, 2)
+        floor_(2, 0, 2)
+        take_max(0, 3, 3)
+        floor_(2, 1, 3)
         round_h(0)
-        base(2, (2, 3))
-        floor_(2, (0, 1))
-        for a in range(PASSES):
-            quantize_w(w5_w, w5_s, w5_b, a, 0)
-        take_min(1, (6, 7))
-        take_max(1, (4, 5))
-        round_h(1)
+        quantize_w5(0)
+        take_min(1, 0, 4)
+        direct(0, 0, 4)
+        take_min(1, 1, 5)
+        direct(0, 1, 5)
+        take_max(1, 0, 0)
+        direct(1, 0, 0)
         quantize_h(0)
-        for a in range(PASSES):
-            quantize_w(w5_w, w5_s, w5_b, a, 1)
-        direct(0, (6, 7))
-        second(0, (6, 7))
-        base(3, (4, 5))
-        take_min(2, (2, 3))
+        finish(0, 0, 4)
+        finish(0, 1, 5)
+        quantize_w5(1)
+        take_max(1, 1, 6)
+        round_h(1)
+        direct(0, 2, 4)
+        finish(0, 2, 4)
+        direct(0, 3, 6)
+        finish(0, 3, 6)
+        direct(1, 1, 5)
+        take_min(2, 0, 1)
+        take_min(2, 1, 7)
+        take_max(2, 0, 2)
         quantize_h(1)
-        store_words(0)
-        floor_(3, (2, 3))
-        direct(1, (6, 7))
-        second(1, (6, 7))
-        take_max(2, (0, 1))
+        finish(1, 0, 0)
+        finish(1, 1, 5)
+        direct(2, 0, 2)
+        take_max(2, 1, 3)
         round_h(2)
-        direct(2, (0, 1))
-        take_min(3, (4, 5))
-        direct(3, (4, 5))
         quantize_h(2)
-        second(2, (0, 1))
-        take_max(3, (2, 3))
-        round_h(3)
-        quantize_h(3)
-        second(3, (4, 5))
-        store_words(1)
+        finish(2, 0, 2)
+        direct(2, 1, 3)
+        finish(2, 1, 3)
         for q in range(4):
             nc.sync.dma_start(
                 out=out_3[0, 4 * q : 4 * q + 4, :].bitcast(I32), in_=h_s[32 * q : 32 * q + 4, :].bitcast(I32)

@@ -147,8 +147,10 @@ def tile_list_margin_collar_alert_kernel(
             )
 
         w1_b1 = sb("w1_b1", [P, 4 * H], BF16)
-        w1_b0 = sb("w1_b0", [P, 4 * H], BF16)
-        w1_b = [None, [w1_b1[:, 0 : 2 * H], w1_b1[:, 2 * H : 4 * H]]]
+        w1_b = [
+            [sb("w1_b0_%d" % u, [P, 2 * H], BF16) for u in range(2)],
+            [w1_b1[:, 0 : 2 * H], w1_b1[:, 2 * H : 4 * H]],
+        ]
         w1_w = [sb("w1_w0", [P, H], U32), sb("w1_w1", [P, H], U32)]
         w1_s = [sb("w1_s%d" % a, [P, H], U8) for a in range(PASSES)]
         w5_both = [staged("w5_b0", [P, 4 * N], BF16, 64 * KB), staged("w5_b1", [P, 4 * N], BF16, 80 * KB)]
@@ -156,10 +158,10 @@ def tile_list_margin_collar_alert_kernel(
         w5_w = [sb("w5_w0", [P, N], U32), staged("w5_w1", [P, N], U32, 107 * KB)]
         w5_s = [sb("w5_s%d" % u, [P, N], U8) for u in range(2)]
 
-        def round_w1_first():
-            nc.vector.tensor_copy(
-                w1_b0[:].rearrange("p (t m j) -> p m j t", t=4, j=4),
-                w1_raw0[:].rearrange("p (j m t) -> p m j t", j=4, t=4),
+        def round_w1_first(u, copy):
+            copy(
+                w1_b[0][u][:].rearrange("p (t m j) -> p m j t", t=2, j=4),
+                w1_raw0[:].rearrange("p (j m t) -> p m j t", j=4, t=4)[:, :, :, 2 * u : 2 * u + 2],
             )
 
         def round_w1_second(v):
@@ -173,6 +175,15 @@ def tile_list_margin_collar_alert_kernel(
                 w5_b[a][u][:].rearrange("p (c i j) -> p c j i", i=4, j=4),
                 w5_raw[a][u][:].rearrange("p (j c i) -> p c j i", j=4, i=4),
             )
+
+        def round_w5_pool(a, u):
+            for v in range(2):
+                lo = 128 * v
+                nc.gpsimd.tensor_scalar(
+                    w5_b[a][u][:, 512 * v : 512 * (v + 1)].rearrange("p (c j) -> p c j", j=4),
+                    w5_raw[a][u][:].rearrange("p (j c) -> p c j", j=4)[:, lo : lo + 128, :],
+                    1.0, 0.0, ALU.mult, ALU.add,
+                )
 
         def quantize_w(words, scales, rounded, a, u):
             cols = slice(256 * u, 256 * (u + 1))
@@ -198,12 +209,10 @@ def tile_list_margin_collar_alert_kernel(
             per_bank = BANK // WIDTHS[c]
             return range(per_bank * u, per_bank * (u + 1))
 
-        def table_passes(words, scales, c, u, bank, closes, order=(0, 1), only=(0, 1)):
+        def table_passes(words, scales, c, u, bank, closes, order=(0, 1)):
             width, lo = WIDTHS[c], STARTS[c] % HALF
             tiles = tiles_of(c, u)
             for a in order:
-                if a not in only:
-                    continue
                 for s, t in enumerate(tiles):
                     cols = slice(P * t, P * (t + 1))
                     nc.tensor.matmul_mx(
@@ -217,7 +226,10 @@ def tile_list_margin_collar_alert_kernel(
                     )
 
         w3_planes = [w3_s[4 * a : P, :] for a in range(PASSES)]
-        cap = [sb("cap%d" % h, [P, 4, HALF], F32) for h in range(2)]
+        cap = [
+            [sb("cap00", [P, 2, HALF], F32), staged("cap01", [P, 2, HALF], F32, 87 * KB)],
+            [staged("cap1%d" % u, [P, 2, HALF], F32, (91 + 4 * u) * KB) for u in range(2)],
+        ]
 
         def chunk_tiles(name, dtype, places):
             return [
@@ -267,7 +279,7 @@ def tile_list_margin_collar_alert_kernel(
             nc.vector.tensor_tensor(
                 low[c][u][:].rearrange("p (s j) -> p s j", j=width),
                 banks[b][:].rearrange("p (s j) -> p s j", j=width),
-                cap[STARTS[c] // HALF][:, tiles.start : tiles.stop, lo : lo + width],
+                cap[STARTS[c] // HALF][tiles.start // 2][:, tiles.start % 2 : (tiles.stop - 1) % 2 + 1, lo : lo + width],
                 ALU.min,
             )
 
@@ -351,8 +363,8 @@ def tile_list_margin_collar_alert_kernel(
         for h in range(2):
             for t in range(4):
                 cap_pass(1, h, t)
-        for b in range(8):
-            nc.scalar.copy(cap[b // 4][:, b % 4, :], banks[b][:])
+        for b in range(2):
+            nc.scalar.copy(cap[0][0][:, b, :], banks[b][:])
         load_w5(1)
         for q in range(4):
             nc.sync.dma_start(
@@ -362,22 +374,26 @@ def tile_list_margin_collar_alert_kernel(
         deal(w3_s[:], w3s_raw[:])
         for a in range(PASSES):
             deal(w3_w[a][:], w3_raw[:, H * a : H * (a + 1)])
+        round_w1_first(0, nc.scalar.copy)
+        round_w1_first(1, nc.vector.tensor_copy)
+        for b in range(2, 8):
+            nc.scalar.copy(cap[b // 4][b // 2 % 2][:, b % 2, :], banks[b][:])
         for t in range(4):
             floor_(0, t, t)
-        round_w1_first()
-        nc.vector.quantize_mx(out=w1_w[0][:].bitcast(FP8X4), scales=w1_s[0][:], in_=w1_b0[:])
-        for v in range(2):
-            round_w1_second(v)
+        quantize_w(w1_w, w1_s, w1_b, 0, 1)
+        round_w1_second(0)
+        quantize_w(w1_w, w1_s, w1_b, 0, 0)
+        round_w1_second(1)
         for u in range(2):
             quantize_w(w1_w, w1_s, w1_b, 1, u)
         nc.sync.dma_start(out=w4_w[:].bitcast(I32), in_=w4_words[0].bitcast(I32))
-        for a in range(PASSES):
-            for t in range(4):
-                table_passes(w1_w, w1_s, 0, t, banks[4 + t], True, (0, 1), (a,))
+        for t in range(4):
+            table_passes(w1_w, w1_s, 0, t, banks[4 + t], True, (1, 0) if t else (0, 1))
 
-        for u in range(2):
-            for a in range(PASSES):
-                round_w5(a, u)
+        for a in range(PASSES):
+            round_w5(a, 0)
+        round_w5(0, 1)
+        round_w5_pool(1, 1)
         take_min(0, 0, 4)
         base(1, 0, 4)
         take_min(0, 1, 5)
@@ -421,10 +437,10 @@ def tile_list_margin_collar_alert_kernel(
         finish(1, 1, 5)
         direct(2, 0, 2)
         take_max(2, 1, 3)
+        direct(2, 1, 3)
         round_h(2)
         quantize_h(2)
         finish(2, 0, 2)
-        direct(2, 1, 3)
         finish(2, 1, 3)
         for q in range(4):
             nc.sync.dma_start(

@@ -20,7 +20,8 @@ P = 128
 PASSES = 2
 HALF = 512
 BANK = 512
-WIDTHS = (512, 256, 256)
+WIDTHS = (512, 512)
+SPLIT = 344
 STARTS = tuple(sum(WIDTHS[:c]) for c in range(len(WIDTHS)))
 
 
@@ -155,7 +156,7 @@ def tile_list_margin_collar_alert_kernel(
         w1_s = [sb("w1_s%d" % a, [P, H], U8) for a in range(PASSES)]
         w5_both = [staged("w5_b0", [P, 4 * N], BF16, 64 * KB), staged("w5_b1", [P, 4 * N], BF16, 80 * KB)]
         w5_b = [[w5_both[u][:, 2 * N * a : 2 * N * (a + 1)] for u in range(2)] for a in range(PASSES)]
-        w5_w = [sb("w5_w0", [P, N], U32), staged("w5_w1", [P, N], U32, 107 * KB)]
+        w5_w = [sb("w5_w0", [P, N], U32), sb("w5_w1", [P, N], U32)]
         w5_s = [sb("w5_s%d" % u, [P, N], U8) for u in range(2)]
 
         def round_w1_first(u, copy):
@@ -242,8 +243,8 @@ def tile_list_margin_collar_alert_kernel(
         hb = chunk_tiles("hb", BF16, {0: 104})
         low = [
             [sb("low0_%d" % u, [P, BANK], F32) for u in range(4)],
-            [sb("low1_%d" % u, [P, BANK], F32) for u in range(2)],
-            [staged("low2_%d" % u, [P, BANK], F32, (103 + 2 * u) * KB) for u in range(2)],
+            [sb("low1_%d" % u, [P, BANK], F32) for u in range(2)]
+            + [sb("low1_2", [P, BANK], F32), staged("low1_3", [P, BANK], F32, 105 * KB)],
         ]
         hf = chunk_tiles("hf", F32, {})
         y = [sb("y%d" % c, [P, 4 * w], F32) for c, w in enumerate(WIDTHS)]
@@ -287,27 +288,24 @@ def tile_list_margin_collar_alert_kernel(
             cols = slice(BANK * u, BANK * (u + 1))
             nc.vector.tensor_tensor(hf[c][:, cols], banks[b][:], low[c][u][:], ALU.max)
             if u % 2:
-                rows = slice(u - 1, u + 1) if c == 0 else slice(0, 4)
+                rows = slice(u - 1, u + 1)
                 nc.sync.dma_start(
                     out=h_rows[:, rows, STARTS[c] : STARTS[c] + WIDTHS[c]],
                     in_=hf[c][:].rearrange("p (t j) -> p t j", t=4)[:, rows, :],
                 )
 
-        def round_h(c):
-            copy = nc.vector.tensor_copy if c == len(WIDTHS) - 1 else nc.scalar.copy
+        def round_h(c, copy, lo, hi):
             copy(
-                hb[c][:].rearrange("p (c i t) -> p c t i", i=4, t=4),
-                hf[c][:].rearrange("p (t c i) -> p c t i", t=4, i=4),
+                hb[c][:].rearrange("p (c i t) -> p c t i", i=4, t=4)[:, lo // 4 : hi // 4, :, :],
+                hf[c][:].rearrange("p (t c i) -> p c t i", t=4, i=4)[:, lo // 4 : hi // 4, :, :],
             )
 
         def quantize_h(c):
             cols = slice(STARTS[c], STARTS[c] + WIDTHS[c])
             nc.vector.quantize_mx(out=h_w[:, cols].bitcast(FP8X4), scales=h_s[:, cols], in_=hb[c][:])
-            if c != 1:
-                half = slice(HALF * (c // 2), HALF * (c // 2 + 1))
-                nc.sync.dma_start(
-                    out=out_2[0].rearrange("p m t -> p (m t)").bitcast(I32)[:, half], in_=h_w[:, half].bitcast(I32)
-                )
+            nc.sync.dma_start(
+                out=out_2[0].rearrange("p m t -> p (m t)").bitcast(I32)[:, cols], in_=h_w[:, cols].bitcast(I32)
+            )
 
         def finish(c, u, b):
             width = WIDTHS[c]
@@ -371,14 +369,13 @@ def tile_list_margin_collar_alert_kernel(
                 out=w4_s[32 * q : 32 * q + 4, :].bitcast(I32),
                 in_=w4_scales[0, 4 * q : 4 * q + 4, :].bitcast(I32),
             )
-        deal(w3_s[:], w3s_raw[:])
-        for a in range(PASSES):
-            deal(w3_w[a][:], w3_raw[:, H * a : H * (a + 1)])
+        for dst, raw in ((w3_w[0][:], w3_raw[:, 0:H]), (w3_s[:], w3s_raw[:]), (w3_w[1][:], w3_raw[:, H : 2 * H])):
+            nc.gpsimd.tensor_copy(dst.rearrange("p (t m) -> p t m", t=4), raw.rearrange("p (m t) -> p t m", t=4))
         round_w1_first(0, nc.scalar.copy)
         round_w1_first(1, nc.vector.tensor_copy)
         for b in range(2, 8):
             nc.scalar.copy(cap[b // 4][b // 2 % 2][:, b % 2, :], banks[b][:])
-        for t in range(4):
+        for t in range(3):
             floor_(0, t, t)
         quantize_w(w1_w, w1_s, w1_b, 0, 1)
         round_w1_second(0)
@@ -388,60 +385,47 @@ def tile_list_margin_collar_alert_kernel(
             quantize_w(w1_w, w1_s, w1_b, 1, u)
         nc.sync.dma_start(out=w4_w[:].bitcast(I32), in_=w4_words[0].bitcast(I32))
         for t in range(4):
-            table_passes(w1_w, w1_s, 0, t, banks[4 + t], True, (1, 0) if t else (0, 1))
+            table_passes(w1_w, w1_s, 0, t, banks[3 + t], True, (1, 0) if t else (0, 1))
+        floor_(0, 3, 7)
 
         for a in range(PASSES):
             round_w5(a, 0)
         round_w5(0, 1)
         round_w5_pool(1, 1)
-        take_min(0, 0, 4)
-        base(1, 0, 4)
-        take_min(0, 1, 5)
-        base(1, 1, 5)
-        take_max(0, 0, 0)
-        floor_(1, 0, 0)
-        take_min(0, 2, 6)
-        floor_(1, 1, 6)
-        take_max(0, 1, 1)
-        base(2, 0, 1)
-        take_min(0, 3, 7)
-        base(2, 1, 7)
-        take_max(0, 2, 2)
-        floor_(2, 0, 2)
-        take_max(0, 3, 3)
-        floor_(2, 1, 3)
-        round_h(0)
+        steps = (
+            (take_min, 0, 3), (take_min, 1, 4), (take_max, 0, 0), (take_min, 2, 5),
+            (take_max, 1, 1), (take_min, 3, 6), (take_max, 2, 2), (take_max, 3, 7),
+        )
+        for take, t, b in steps:
+            take(0, t, b)
+            (base if take is take_min else floor_)(1, t, b)
+        round_h(0, nc.scalar.copy, 0, HALF)
         quantize_w5(0)
-        take_min(1, 0, 4)
-        direct(0, 0, 4)
-        take_min(1, 1, 5)
-        direct(0, 1, 5)
-        take_max(1, 0, 0)
-        direct(1, 0, 0)
-        quantize_h(0)
-        finish(0, 0, 4)
-        finish(0, 1, 5)
+        take_min(1, 0, 3)
+        direct(0, 0, 3)
+        take_min(1, 1, 4)
+        direct(0, 1, 4)
         quantize_w5(1)
-        take_max(1, 1, 6)
-        round_h(1)
-        direct(0, 2, 4)
-        finish(0, 2, 4)
-        direct(0, 3, 6)
-        finish(0, 3, 6)
-        direct(1, 1, 5)
-        take_min(2, 0, 1)
-        take_min(2, 1, 7)
-        take_max(2, 0, 2)
+        take_max(1, 0, 0)
+        direct(0, 2, 0)
+        take_min(1, 2, 5)
+        direct(0, 3, 5)
+        quantize_h(0)
+        for n, b in enumerate((3, 4, 0, 5)):
+            finish(0, n, b)
+        direct(1, 0, 3)
+        direct(1, 1, 4)
+        take_max(1, 1, 1)
+        direct(1, 2, 1)
+        take_min(1, 3, 6)
+        direct(1, 3, 6)
+        take_max(1, 2, 2)
+        take_max(1, 3, 7)
+        round_h(1, nc.vector.tensor_copy, 0, SPLIT)
+        round_h(1, nc.scalar.copy, SPLIT, HALF)
         quantize_h(1)
-        finish(1, 0, 0)
-        finish(1, 1, 5)
-        direct(2, 0, 2)
-        take_max(2, 1, 3)
-        direct(2, 1, 3)
-        round_h(2)
-        quantize_h(2)
-        finish(2, 0, 2)
-        finish(2, 1, 3)
+        for n, b in enumerate((3, 4, 1, 6)):
+            finish(1, n, b)
         for q in range(4):
             nc.sync.dma_start(
                 out=out_3[0, 4 * q : 4 * q + 4, :].bitcast(I32), in_=h_s[32 * q : 32 * q + 4, :].bitcast(I32)

@@ -21,7 +21,7 @@ PASSES = 2
 HALF = 512
 BANK = 512
 WIDTHS = (512, 512)
-SPLIT = 344
+PARTS = ((0, 512), (512, 256), (768, 256))
 STARTS = tuple(sum(WIDTHS[:c]) for c in range(len(WIDTHS)))
 
 
@@ -244,10 +244,10 @@ def tile_list_margin_collar_alert_kernel(
         low = [
             [sb("low0_%d" % u, [P, BANK], F32) for u in range(4)],
             [sb("low1_%d" % u, [P, BANK], F32) for u in range(2)]
-            + [sb("low1_2", [P, BANK], F32), staged("low1_3", [P, BANK], F32, 105 * KB)],
+            + [staged("low1_%d" % (2 + u), [P, BANK], F32, (103 + 2 * u) * KB) for u in range(2)],
         ]
         hf = chunk_tiles("hf", F32, {})
-        y = [sb("y%d" % c, [P, 4 * w], F32) for c, w in enumerate(WIDTHS)]
+        y = [sb("y%d" % c, [P, 4 * w], F32) for c, (first, w) in enumerate(PARTS)]
         h_w = sb("h_w", [P, S], U32)
         h_s = sb("h_s", [P, S], U8)
         h_rows = out_1.rearrange("(p t) j -> p t j", t=4)
@@ -259,17 +259,22 @@ def tile_list_margin_collar_alert_kernel(
         def base(c, u, b):
             table_passes(w1_w, w1_s, c, u, banks[b], True, (1, 0))
 
-        def direct(c, u, b):
-            width, lo = WIDTHS[c], STARTS[c] % HALF
+        def part_tiles(e, u):
+            per_bank = BANK // PARTS[e][1]
+            return range(per_bank * u, per_bank * (u + 1))
+
+        def direct(e, u, b):
+            first, width = PARTS[e]
+            lo = first % HALF
             for a in range(PASSES):
-                for s, n in enumerate(tiles_of(c, u)):
+                for s, n in enumerate(part_tiles(e, u)):
                     cols = slice(256 * a + P * (n % 2), 256 * a + P * (n % 2 + 1))
                     nc.tensor.matmul_mx(
                         out=banks[b][:, width * s : width * (s + 1)],
                         lhsT=w5_w[n // 2][:, cols].bitcast(FP8X4),
                         lhsT_scale=w5_s[n // 2][:, cols],
-                        rhs=g_w[a][STARTS[c] // HALF][:, lo : lo + width].bitcast(FP8X4),
-                        rhs_scale=planes[a][:, STARTS[c] : STARTS[c] + width],
+                        rhs=g_w[a][first // HALF][:, lo : lo + width].bitcast(FP8X4),
+                        rhs_scale=planes[a][:, first : first + width],
                         start=(a == 0 and s == 0),
                         stop=False,
                     )
@@ -287,8 +292,8 @@ def tile_list_margin_collar_alert_kernel(
         def take_max(c, u, b):
             cols = slice(BANK * u, BANK * (u + 1))
             nc.vector.tensor_tensor(hf[c][:, cols], banks[b][:], low[c][u][:], ALU.max)
-            if u % 2:
-                rows = slice(u - 1, u + 1)
+            if u % 2 or (c, u) == (1, 0):
+                rows = slice(u, u + 1) if c == 1 and u < 2 else slice(u - 1, u + 1)
                 nc.sync.dma_start(
                     out=h_rows[:, rows, STARTS[c] : STARTS[c] + WIDTHS[c]],
                     in_=hf[c][:].rearrange("p (t j) -> p t j", t=4)[:, rows, :],
@@ -300,20 +305,26 @@ def tile_list_margin_collar_alert_kernel(
                 hf[c][:].rearrange("p (t c i) -> p c t i", t=4, i=4)[:, lo // 4 : hi // 4, :, :],
             )
 
-        def quantize_h(c):
-            cols = slice(STARTS[c], STARTS[c] + WIDTHS[c])
-            nc.vector.quantize_mx(out=h_w[:, cols].bitcast(FP8X4), scales=h_s[:, cols], in_=hb[c][:])
-            nc.sync.dma_start(
-                out=out_2[0].rearrange("p m t -> p (m t)").bitcast(I32)[:, cols], in_=h_w[:, cols].bitcast(I32)
+        def quantize_h(e):
+            first, width = PARTS[e]
+            cols = slice(first, first + width)
+            lo = 4 * (first % HALF)
+            nc.vector.quantize_mx(
+                out=h_w[:, cols].bitcast(FP8X4), scales=h_s[:, cols], in_=hb[first // HALF][:, lo : lo + 4 * width]
             )
+            if (first + width) % HALF == 0:
+                half = slice(first + width - HALF, first + width)
+                nc.sync.dma_start(
+                    out=out_2[0].rearrange("p m t -> p (m t)").bitcast(I32)[:, half], in_=h_w[:, half].bitcast(I32)
+                )
 
-        def finish(c, u, b):
-            width = WIDTHS[c]
+        def finish(e, u, b):
+            first, width = PARTS[e]
             step = BANK if width == BANK else P
-            tiles = tiles_of(c, u)
+            tiles = part_tiles(e, u)
             for s, n in enumerate(tiles):
                 for k in range(width // step):
-                    cols = slice(STARTS[c] + step * k, STARTS[c] + step * (k + 1))
+                    cols = slice(first + step * k, first + step * (k + 1))
                     nc.tensor.matmul_mx(
                         out=banks[b][:, width * s + step * k : width * s + step * (k + 1)],
                         lhsT=w4_w[:, 256 * n : 256 * (n + 1)].bitcast(FP4X4),
@@ -324,10 +335,10 @@ def tile_list_margin_collar_alert_kernel(
                         stop=(s == len(tiles) - 1 and k == width // step - 1),
                     )
             cols = slice(BANK * u, BANK * (u + 1))
-            nc.scalar.activation(y[c][:, cols], banks[b][:], ACT.Silu)
+            nc.scalar.activation(y[e][:, cols], banks[b][:], ACT.Silu)
             nc.sync.dma_start(
-                out=y_rows[:, tiles.start : tiles.stop, STARTS[c] : STARTS[c] + width],
-                in_=y[c][:, cols].rearrange("p (s j) -> p s j", j=width),
+                out=y_rows[:, tiles.start : tiles.stop, first : first + width],
+                in_=y[e][:, cols].rearrange("p (s j) -> p s j", j=width),
             )
 
         nc.vector.tensor_copy(g_s[:], tab_s[:].indirect(offsets[:]))
@@ -408,24 +419,29 @@ def tile_list_margin_collar_alert_kernel(
         quantize_w5(1)
         take_max(1, 0, 0)
         direct(0, 2, 0)
+        quantize_h(0)
+        finish(0, 0, 3)
+        finish(0, 1, 4)
+        finish(0, 2, 0)
         take_min(1, 2, 5)
         direct(0, 3, 5)
-        quantize_h(0)
-        for n, b in enumerate((3, 4, 0, 5)):
-            finish(0, n, b)
+        finish(0, 3, 5)
         direct(1, 0, 3)
         direct(1, 1, 4)
         take_max(1, 1, 1)
-        direct(1, 2, 1)
+        direct(2, 0, 1)
         take_min(1, 3, 6)
-        direct(1, 3, 6)
+        direct(2, 1, 6)
         take_max(1, 2, 2)
         take_max(1, 3, 7)
-        round_h(1, nc.vector.tensor_copy, 0, SPLIT)
-        round_h(1, nc.scalar.copy, SPLIT, HALF)
+        round_h(1, nc.vector.tensor_copy, 0, 256)
+        round_h(1, nc.scalar.copy, 256, HALF)
         quantize_h(1)
-        for n, b in enumerate((3, 4, 1, 6)):
-            finish(1, n, b)
+        finish(1, 0, 3)
+        finish(1, 1, 4)
+        quantize_h(2)
+        finish(2, 0, 1)
+        finish(2, 1, 6)
         for q in range(4):
             nc.sync.dma_start(
                 out=out_3[0, 4 * q : 4 * q + 4, :].bitcast(I32), in_=h_s[32 * q : 32 * q + 4, :].bitcast(I32)

from contextlib import ExitStack

import concourse.mybir as mybir

K, H, N, T, S = 1024, 512, 512, 2048, 1024
FLOPS = 2 * S * (3 * K * H + H * N + K * N)

F32 = mybir.dt.float32
BF16 = mybir.dt.bfloat16
I32 = mybir.dt.int32
U32 = mybir.dt.uint32
U16 = mybir.dt.uint16
U8 = mybir.dt.uint8
FP8X4 = mybir.dt.float8_e4m3fn_x4
FP4X4 = mybir.dt.float4_e2m1fn_x4
ALU = mybir.AluOpType
ACT = mybir.ActivationFunctionType

P = 128
PASSES = 2
HALF = 512
BANK = 512
WIDTHS = (512, 512)
PARTS = ((0, 512), (512, 256), (768, 256))
STARTS = tuple(sum(WIDTHS[:c]) for c in range(len(WIDTHS)))


def tile_list_margin_collar_alert_kernel(
    tc, tab_words, tab_scales, offs, w1, w2_words, w2_scales, w3_words, w3_scales,
    w4_words, w4_scales, w5, out_0, out_1, out_2, out_3,
):
    nc = tc.nc
    with ExitStack() as ctx:
        keep = ctx.enter_context(tc.tile_pool(name="keep", bufs=1))
        psum = ctx.enter_context(tc.psum_pool(name="psum", bufs=1))

        def sb(name, shape, dtype):
            return keep.tile(shape, dtype, name=name, align_bytes=64)

        offsets = keep.tile([P, S // 16], U16, name="offsets")
        nc.sync.dma_start(offsets[:], offs)

        banks = [psum.tile([P, BANK], F32, name="bank%d" % b) for b in range(8)]
        g_s = sb("g_s", [P, S], U8)
        gs_low = sb("gs_low", [P, S], U8)
        warm = sb("warm", [P, 8], F32)

        stage = ctx.enter_context(tc.tile_pool(name="stage", bufs=1))

        def staged(name, shape, dtype, at):
            return stage.tile(shape, dtype, name=name, offset=at, align_bytes=64)

        KB = 1024
        tab_s = staged("tab_s", [P, T], U8, 97 * KB + 512)
        zeros_a = staged("zeros_a", [P, 256], I32, 11 * KB)
        zeros_b = staged("zeros_b", [P, 256], I32, 34 * KB - 512)
        tab_w = [staged("tab_w0", [P, T], I32, 4 * KB), staged("tab_w1", [P, T], I32, 26 * KB)]
        w2_raw = staged("w2_raw", [P, PASSES * 2 * H], U8, 13 * KB)
        w3_raw = staged("w3_raw", [P, PASSES * H], I32, 34 * KB)
        w2s_raw = staged("w2s_raw", [P, PASSES * H], U8, 46 * KB)
        w3s_raw = sb("w3s_raw", [P, H], U8)
        g_w01 = staged("g_w01", [P, HALF], U32, 46 * KB + 512)
        w1_raw0 = staged("w1_raw0", [P, 4 * H], F32, 90 * KB)
        w1_raw1 = [
            staged("w1_raw1_0", [P, 2 * H], F32, 99 * KB),
            staged("w1_raw1_1", [P, 2 * H], F32, 42 * KB + 512),
        ]
        w5_raw = [
            [staged("w5_raw%d_%d" % (a, u), [P, 2 * N], F32, (4 + 4 * a + 22 * u) * KB) for u in range(2)]
            for a in range(PASSES)
        ]
        w4_w = staged("w4_w", [P, 2 * N], U8, 43 * KB)

        nc.vector.memset(tab_s[:].bitcast(I32), 0)
        nc.vector.memset(zeros_a[:], 0)
        nc.vector.tensor_copy(w2s_raw[:].bitcast(I32), zeros_a[:])
        nc.vector.memset(zeros_b[:], 0)
        nc.vector.tensor_copy(gs_low[:].bitcast(I32), zeros_b[:])
        nc.vector.tensor_copy(w3s_raw[:].bitcast(I32), zeros_b[:, 0:128])
        nc.gpsimd.memset(warm[:, 0:4], 0.0)
        nc.scalar.activation(warm[:, 4:8], warm[:, 0:4], ACT.Silu)

        def load_words(tile, words):
            nc.sync.dma_start(out=tile[:], in_=words.rearrange("p t i -> p (t i)").bitcast(I32))

        def load_rows(tile, w, a):
            nc.sync.dma_start(
                out=tile[:], in_=w[512 * a : 512 * (a + 1), :].rearrange("(p j) c -> p (j c)", j=4)
            )

        nc.sync.dma_start(
            out=w2_raw[:].bitcast(I32).rearrange("p (a c) -> p a c", a=PASSES),
            in_=w2_words.rearrange("a p c -> p a c").bitcast(I32),
        )
        def load_w1_second(v):
            rows = w1[512:1024, :].rearrange("(p j) c -> p j c", j=4)
            nc.sync.dma_start(
                out=w1_raw1[v][:].rearrange("p (j c) -> p j c", j=4), in_=rows[:, :, 256 * v : 256 * (v + 1)]
            )

        def load_w5(u):
            for a in range(PASSES):
                rows = w5[512 * a : 512 * (a + 1), :].rearrange("(p j) c -> p j c", j=4)
                nc.sync.dma_start(
                    out=w5_raw[a][u][:].rearrange("p (j c) -> p j c", j=4), in_=rows[:, :, 256 * u : 256 * (u + 1)]
                )

        ts_rows = tab_scales.rearrange("a (q r) t -> r q a t", r=4)
        for r in range(4):
            nc.sync.dma_start(out=tab_s[r:P:16, :].bitcast(I32), in_=ts_rows[r].bitcast(I32))
        load_words(tab_w[0], tab_words[0])
        for q in range(4):
            nc.sync.dma_start(
                out=w2s_raw[32 * q : 32 * q + 4, :].bitcast(I32).rearrange("r (a c) -> r a c", a=PASSES),
                in_=w2_scales[:, 4 * q : 4 * q + 4, :].rearrange("a r c -> r a c").bitcast(I32),
            )
        load_words(tab_w[1], tab_words[1])
        nc.sync.dma_start(
            out=w3_raw[:].rearrange("p (a c) -> p a c", a=PASSES),
            in_=w3_words.rearrange("a p c i -> p a (c i)").bitcast(I32),
        )
        for q in range(4):
            nc.sync.dma_start(
                out=w3s_raw[32 * q : 32 * q + 8, :].bitcast(I32),
                in_=w3_scales[:, 4 * q : 4 * q + 4, :].bitcast(I32),
            )

        g_w = [
            [staged("g_w00", [P, HALF], U32, 72 * KB), g_w01],
            [sb("g_w10", [P, HALF], U32), sb("g_w11", [P, HALF], U32)],
        ]
        planes = [g_s, gs_low]

        def gather_words(a, h):
            nc.vector.tensor_copy(
                g_w[a][h][:], tab_w[a][:].bitcast(U32).indirect(offsets[:, 32 * h : 32 * (h + 1)])
            )

        w3_s = sb("w3_s", [P, H], U8)
        ws = [sb("ws%d" % a, [P, H], U8) for a in range(PASSES)]
        w3_w = [sb("w3_w0", [P, H], I32), sb("w3_w1", [P, H], I32)]
        w2_w = [sb("w2_w0", [P, 2 * H], U8), staged("w2_w1", [P, 2 * H], U8, 76 * KB)]
        w4_s = ws[1]

        def deal(dst, src):
            nc.vector.tensor_copy(
                dst.rearrange("p (a t m) -> p a m t", t=4, m=P), src.rearrange("p (a m t) -> p a m t", t=4, m=P)
            )

        w1_b1 = sb("w1_b1", [P, 4 * H], BF16)
        w1_b = [
            [sb("w1_b0_%d" % u, [P, 2 * H], BF16) for u in range(2)],
            [w1_b1[:, 0 : 2 * H], w1_b1[:, 2 * H : 4 * H]],
        ]
        w1_w = [sb("w1_w0", [P, H], U32), sb("w1_w1", [P, H], U32)]
        w1_s = [sb("w1_s%d" % a, [P, H], U8) for a in range(PASSES)]
        w5_both = [staged("w5_b0", [P, 4 * N], BF16, 64 * KB), staged("w5_b1", [P, 4 * N], BF16, 80 * KB)]
        w5_b = [[w5_both[u][:, 2 * N * a : 2 * N * (a + 1)] for u in range(2)] for a in range(PASSES)]
        w5_w = [sb("w5_w0", [P, N], U32), sb("w5_w1", [P, N], U32)]
        w5_s = [sb("w5_s%d" % u, [P, N], U8) for u in range(2)]

        def round_w1_first(u, copy):
            copy(
                w1_b[0][u][:].rearrange("p (t m j) -> p m j t", t=2, j=4),
                w1_raw0[:].rearrange("p (j m t) -> p m j t", j=4, t=4)[:, :, :, 2 * u : 2 * u + 2],
            )

        def round_w1_second(v):
            nc.vector.tensor_copy(
                w1_b1[:].rearrange("p (t m j) -> p m j t", t=4, j=4)[:, 64 * v : 64 * (v + 1), :, :],
                w1_raw1[v][:].rearrange("p (j m t) -> p m j t", j=4, t=4),
            )

        def round_w5(a, u):
            nc.scalar.copy(
                w5_b[a][u][:].rearrange("p (c i j) -> p c j i", i=4, j=4),
                w5_raw[a][u][:].rearrange("p (j c i) -> p c j i", j=4, i=4),
            )

        def round_w5_pool(a, u):
            for v in range(2):
                lo = 128 * v
                nc.gpsimd.tensor_scalar(
                    w5_b[a][u][:, 512 * v : 512 * (v + 1)].rearrange("p (c j) -> p c j", j=4),
                    w5_raw[a][u][:].rearrange("p (j c) -> p c j", j=4)[:, lo : lo + 128, :],
                    1.0, 0.0, ALU.mult, ALU.add,
                )

        def quantize_w(words, scales, rounded, a, u):
            cols = slice(256 * u, 256 * (u + 1))
            nc.vector.quantize_mx(
                out=words[a][:, cols].bitcast(FP8X4), scales=scales[a][:, cols], in_=rounded[a][u][:]
            )

        def quantize_w5(u):
            nc.vector.quantize_mx(out=w5_w[u][:].bitcast(FP8X4), scales=w5_s[u][:], in_=w5_both[u][:])

        def cap_pass(a, h, t):
            nc.tensor.matmul_mx(
                out=banks[4 * h + t][:],
                lhsT=w2_w[a][:, 256 * t : 256 * (t + 1)].bitcast(FP4X4),
                lhsT_scale=ws[a][:, P * t : P * (t + 1)],
                rhs=g_w[a][h][:].bitcast(FP8X4),
                rhs_scale=planes[a][:, HALF * h : HALF * (h + 1)],
                start=(a == 0),
                stop=(a == PASSES - 1),
            )

        def tiles_of(c, u):
            per_bank = BANK // WIDTHS[c]
            return range(per_bank * u, per_bank * (u + 1))

        def table_passes(words, scales, c, u, bank, closes, order=(0, 1)):
            width, lo = WIDTHS[c], STARTS[c] % HALF
            tiles = tiles_of(c, u)
            for a in order:
                for s, t in enumerate(tiles):
                    cols = slice(P * t, P * (t + 1))
                    nc.tensor.matmul_mx(
                        out=bank[:, width * s : width * (s + 1)],
                        lhsT=words[a][:, cols].bitcast(FP8X4),
                        lhsT_scale=scales[a][:, cols],
                        rhs=g_w[a][STARTS[c] // HALF][:, lo : lo + width].bitcast(FP8X4),
                        rhs_scale=planes[a][:, STARTS[c] : STARTS[c] + width],
                        start=(a == order[0] and s == 0),
                        stop=(closes and a == order[-1] and s == len(tiles) - 1),
                    )

        w3_planes = [w3_s[4 * a : P, :] for a in range(PASSES)]
        cap = [
            [sb("cap00", [P, 2, HALF], F32), staged("cap01", [P, 2, HALF], F32, 87 * KB)],
            [staged("cap1%d" % u, [P, 2, HALF], F32, (91 + 4 * u) * KB) for u in range(2)],
        ]

        def chunk_tiles(name, dtype, places):
            return [
                staged("%s%d" % (name, c), [P, 4 * w], dtype, places[c] * KB)
                if c in places
                else sb("%s%d" % (name, c), [P, 4 * w], dtype)
                for c, w in enumerate(WIDTHS)
            ]

        hb = chunk_tiles("hb", BF16, {0: 104})
        low = [
            [sb("low0_%d" % u, [P, BANK], F32) for u in range(4)],
            [sb("low1_%d" % u, [P, BANK], F32) for u in range(2)]
            + [staged("low1_%d" % (2 + u), [P, BANK], F32, (103 + 2 * u) * KB) for u in range(2)],
        ]
        hf = chunk_tiles("hf", F32, {})
        y = [sb("y%d" % c, [P, 4 * w], F32) for c, (first, w) in enumerate(PARTS)]
        h_w = sb("h_w", [P, S], U32)
        h_s = sb("h_s", [P, S], U8)
        h_rows = out_1.rearrange("(p t) j -> p t j", t=4)
        y_rows = out_0.rearrange("(u p) j -> p u j", p=P)

        def floor_(c, u, b):
            table_passes(w3_w, w3_planes, c, u, banks[b], True)

        def base(c, u, b):
            table_passes(w1_w, w1_s, c, u, banks[b], True, (1, 0))

        def part_tiles(e, u):
            per_bank = BANK // PARTS[e][1]
            return range(per_bank * u, per_bank * (u + 1))

        def direct(e, u, b):
            first, width = PARTS[e]
            lo = first % HALF
            for a in range(PASSES):
                for s, n in enumerate(part_tiles(e, u)):
                    cols = slice(256 * a + P * (n % 2), 256 * a + P * (n % 2 + 1))
                    nc.tensor.matmul_mx(
                        out=banks[b][:, width * s : width * (s + 1)],
                        lhsT=w5_w[n // 2][:, cols].bitcast(FP8X4),
                        lhsT_scale=w5_s[n // 2][:, cols],
                        rhs=g_w[a][first // HALF][:, lo : lo + width].bitcast(FP8X4),
                        rhs_scale=planes[a][:, first : first + width],
                        start=(a == 0 and s == 0),
                        stop=False,
                    )

        def take_min(c, u, b):
            width, lo = WIDTHS[c], STARTS[c] % HALF
            tiles = tiles_of(c, u)
            nc.vector.tensor_tensor(
                low[c][u][:].rearrange("p (s j) -> p s j", j=width),
                banks[b][:].rearrange("p (s j) -> p s j", j=width),
                cap[STARTS[c] // HALF][tiles.start // 2][:, tiles.start % 2 : (tiles.stop - 1) % 2 + 1, lo : lo + width],
                ALU.min,
            )

        def take_max(c, u, b):
            cols = slice(BANK * u, BANK * (u + 1))
            nc.vector.tensor_tensor(hf[c][:, cols], banks[b][:], low[c][u][:], ALU.max)
            if u % 2 or (c, u) == (1, 0):
                rows = slice(u, u + 1) if c == 1 and u < 2 else slice(u - 1, u + 1)
                nc.sync.dma_start(
                    out=h_rows[:, rows, STARTS[c] : STARTS[c] + WIDTHS[c]],
                    in_=hf[c][:].rearrange("p (t j) -> p t j", t=4)[:, rows, :],
                )

        def round_h(c, copy, lo, hi):
            copy(
                hb[c][:].rearrange("p (c i t) -> p c t i", i=4, t=4)[:, lo // 4 : hi // 4, :, :],
                hf[c][:].rearrange("p (t c i) -> p c t i", t=4, i=4)[:, lo // 4 : hi // 4, :, :],
            )

        def quantize_h(e):
            first, width = PARTS[e]
            cols = slice(first, first + width)
            lo = 4 * (first % HALF)
            nc.vector.quantize_mx(
                out=h_w[:, cols].bitcast(FP8X4), scales=h_s[:, cols], in_=hb[first // HALF][:, lo : lo + 4 * width]
            )
            if (first + width) % HALF == 0:
                half = slice(first + width - HALF, first + width)
                nc.sync.dma_start(
                    out=out_2[0].rearrange("p m t -> p (m t)").bitcast(I32)[:, half], in_=h_w[:, half].bitcast(I32)
                )

        def finish(e, u, b):
            first, width = PARTS[e]
            step = BANK if width == BANK else P
            tiles = part_tiles(e, u)
            for s, n in enumerate(tiles):
                for k in range(width // step):
                    cols = slice(first + step * k, first + step * (k + 1))
                    nc.tensor.matmul_mx(
                        out=banks[b][:, width * s + step * k : width * s + step * (k + 1)],
                        lhsT=w4_w[:, 256 * n : 256 * (n + 1)].bitcast(FP4X4),
                        lhsT_scale=w4_s[:, P * n : P * (n + 1)],
                        rhs=h_w[:, cols].bitcast(FP8X4),
                        rhs_scale=h_s[:, cols],
                        start=False,
                        stop=(s == len(tiles) - 1 and k == width // step - 1),
                    )
            cols = slice(BANK * u, BANK * (u + 1))
            nc.scalar.activation(y[e][:, cols], banks[b][:], ACT.Silu)
            nc.sync.dma_start(
                out=y_rows[:, tiles.start : tiles.stop, first : first + width],
                in_=y[e][:, cols].rearrange("p (s j) -> p s j", j=width),
            )

        nc.vector.tensor_copy(g_s[:], tab_s[:].indirect(offsets[:]))
        nc.sync.dma_start(out=gs_low[0:100, :].bitcast(I32), in_=g_s[16:116, :].bitcast(I32))
        load_rows(w1_raw0, w1, 0)
        load_w1_second(0)
        for i in range(3):
            nc.tensor.matmul_mx(
                out=banks[7][:],
                lhsT=w2_raw[:, 0 : 2 * P].bitcast(FP4X4),
                lhsT_scale=g_s[:, 0:P],
                rhs=tab_w[0][:, 0:HALF].bitcast(FP8X4),
                rhs_scale=g_s[:, 0:HALF],
                start=True,
                stop=True,
            )
        gather_words(0, 0)
        deal(ws[0][:], w2s_raw[:, 0:H])
        deal(w2_w[0][:].bitcast(U16), w2_raw[:, 0 : 2 * H].bitcast(U16))
        for t in range(4):
            cap_pass(0, 0, t)
        deal(w2_w[1][:].bitcast(U16), w2_raw[:, 2 * H : 4 * H].bitcast(U16))
        deal(ws[1][:], w2s_raw[:, H : 2 * H])
        gather_words(0, 1)
        load_w1_second(1)
        load_w5(0)
        for t in range(4):
            cap_pass(0, 1, t)
        gather_words(1, 0)
        gather_words(1, 1)
        for h in range(2):
            for t in range(4):
                cap_pass(1, h, t)
        for b in range(2):
            nc.scalar.copy(cap[0][0][:, b, :], banks[b][:])
        load_w5(1)
        for q in range(4):
            nc.sync.dma_start(
                out=w4_s[32 * q : 32 * q + 4, :].bitcast(I32),
                in_=w4_scales[0, 4 * q : 4 * q + 4, :].bitcast(I32),
            )
        for dst, raw in ((w3_w[0][:], w3_raw[:, 0:H]), (w3_s[:], w3s_raw[:]), (w3_w[1][:], w3_raw[:, H : 2 * H])):
            nc.gpsimd.tensor_copy(dst.rearrange("p (t m) -> p t m", t=4), raw.rearrange("p (m t) -> p t m", t=4))
        round_w1_first(0, nc.scalar.copy)
        round_w1_first(1, nc.vector.tensor_copy)
        for b in range(2, 8):
            nc.scalar.copy(cap[b // 4][b // 2 % 2][:, b % 2, :], banks[b][:])
        for t in range(3):
            floor_(0, t, t)
        quantize_w(w1_w, w1_s, w1_b, 0, 1)
        round_w1_second(0)
        quantize_w(w1_w, w1_s, w1_b, 0, 0)
        round_w1_second(1)
        for u in range(2):
            quantize_w(w1_w, w1_s, w1_b, 1, u)
        nc.sync.dma_start(out=w4_w[:].bitcast(I32), in_=w4_words[0].bitcast(I32))
        for t in range(4):
            table_passes(w1_w, w1_s, 0, t, banks[3 + t], True, (1, 0) if t else (0, 1))
        floor_(0, 3, 7)

        for a in range(PASSES):
            round_w5(a, 0)
        round_w5(0, 1)
        round_w5_pool(1, 1)
        steps = (
            (take_min, 0, 3), (take_min, 1, 4), (take_max, 0, 0), (take_min, 2, 5),
            (take_max, 1, 1), (take_min, 3, 6), (take_max, 2, 2), (take_max, 3, 7),
        )
        for take, t, b in steps:
            take(0, t, b)
            (base if take is take_min else floor_)(1, t, b)
        round_h(0, nc.scalar.copy, 0, HALF)
        quantize_w5(0)
        take_min(1, 0, 3)
        direct(0, 0, 3)
        take_min(1, 1, 4)
        direct(0, 1, 4)
        quantize_w5(1)
        take_max(1, 0, 0)
        direct(0, 2, 0)
        quantize_h(0)
        finish(0, 0, 3)
        finish(0, 1, 4)
        finish(0, 2, 0)
        take_min(1, 2, 5)
        direct(0, 3, 5)
        finish(0, 3, 5)
        direct(1, 0, 3)
        direct(1, 1, 4)
        take_max(1, 1, 1)
        direct(2, 0, 1)
        take_min(1, 3, 6)
        direct(2, 1, 6)
        take_max(1, 2, 2)
        take_max(1, 3, 7)
        round_h(1, nc.vector.tensor_copy, 0, 256)
        round_h(1, nc.scalar.copy, 256, HALF)
        quantize_h(1)
        finish(1, 0, 3)
        finish(1, 1, 4)
        quantize_h(2)
        finish(2, 0, 1)
        finish(2, 1, 6)
        for q in range(4):
            nc.sync.dma_start(
                out=out_3[0, 4 * q : 4 * q + 4, :].bitcast(I32), in_=h_s[32 * q : 32 * q + 4, :].bitcast(I32)
            )
